import numpy as np
import ml_dtypes


def mxq(x, axis, fmt="e4m3"):
    dtype, down = {"e4m3": (ml_dtypes.float8_e4m3fn, 7), "e5m2": (ml_dtypes.float8_e5m2, 14)}[fmt]
    v = np.moveaxis(np.asarray(x, np.float32).astype(ml_dtypes.bfloat16).astype(np.float64), axis, -1)
    blocks = v.reshape(v.shape[:-1] + (-1, 32))
    amax = np.abs(blocks).max(-1, keepdims=True)
    byte = np.maximum(np.where(amax > 0, np.frexp(amax)[1] - 1 + 127, 0) - down, 1)
    scale = np.exp2(byte - 127.0)
    codes = (blocks / scale).astype(np.float32).astype(dtype).astype(np.float64)
    return np.moveaxis((codes * scale).reshape(v.shape), -1, axis)


WIDE = False


def mx_kscale(k):
    if not WIDE:
        return np.ones(k)
    levels = np.array([10, -10, 5, -5, 0])
    if k % 512:
        return np.exp2(np.random.permutation(np.resize(levels, k // 32))).repeat(32)
    a = np.empty((k // 512, 16))
    for p in range(k // 512):
        a[p, :8] = np.random.permutation(np.resize(levels, 8))
        for g in range(8):
            far = levels[np.abs(levels - a[p, g]) >= 10]
            a[p, g + 8] = far[np.random.randint(len(far))]
    return np.exp2(a.ravel()).repeat(32)


def f64(x):
    return np.asarray(x).astype(np.float64)


def striped(idx):
    return np.tile(idx.reshape(-1, 16).T, (8, 1)).astype(np.uint16)


def unstriped(offs):
    return offs[:16].T.reshape(-1).astype(np.int64)


E2M1 = np.array([0.0, 0.5, 1.0, 1.5, 2.0, 3.0, 4.0, 6.0, -0.0, -0.5, -1.0, -1.5, -2.0, -3.0, -4.0, -6.0])


def pack_fp4(w):
    k, n = w.shape
    w = f64(np.asarray(w, np.float32).astype(ml_dtypes.bfloat16)).reshape(k // 32, 32, n)
    amax = np.abs(w).max(1)
    mant, ex = np.frexp(amax / 6.0)
    byte = np.clip(np.where(amax > 0, np.where(mant > 0.5, ex, ex - 1) + 127, 1), 1, 254)
    scaled = (w * np.exp2(127.0 - byte)[:, None, :]).reshape(k, n).astype(np.float32)
    c = np.ascontiguousarray(scaled.reshape(k // 512, 128, 4, n).transpose(0, 1, 3, 2)).astype(ml_dtypes.float4_e2m1fn).view(np.uint8) & 0xF
    words = (c[..., 0::2] | (c[..., 1::2] << 4)).reshape(k // 512, 128, 2 * n)
    return np.ascontiguousarray(words), np.ascontiguousarray(byte.astype(np.uint8).reshape(k // 512, 16, n))


def unpack_fp4(words, scales):
    g, _, n = scales.shape
    words = np.ascontiguousarray(words).reshape(g, 128, n, 2)
    nib = np.empty((g, 128, n, 4), np.uint8)
    nib[..., 0::2] = words & 0xF
    nib[..., 1::2] = words >> 4
    vals = E2M1[nib] * np.repeat(np.exp2(scales.astype(np.float64) - 127.0), 8, axis=1)[..., None]
    return vals.transpose(0, 1, 3, 2).reshape(g * 512, n)


def silu(v):
    return v / (1.0 + np.exp(-np.maximum(v, -700.0)))


K, T, S, V, N = 512, 1024, 512, 256, 256


def setup_inputs():
    n = np.random.standard_normal
    s = mx_kscale(K)[:, None]
    packed_w1 = pack_fp4(n((K, N)) / np.sqrt(K) / s)
    packed_w2 = pack_fp4(n((K, N)) / np.sqrt(K) / s)
    packed_w3 = pack_fp4(n((K, N)) / np.sqrt(K) / s)
    return {
        "xT": (n((K, T)) * s).astype(np.float32),
        "w1_words": packed_w1[0],
        "w1_scales": packed_w1[1],
        "w2_words": packed_w2[0],
        "w2_scales": packed_w2[1],
        "w3_words": packed_w3[0],
        "w3_scales": packed_w3[1],
        "offs": striped(np.random.permutation(T)[:S]),
        "cen": striped(np.random.permutation(S)[:V]),
        "pos1": striped(np.random.permutation(S)[:V]),
        "pos2": striped(np.random.permutation(S)[:V]),
    }


def reference(xT, w1_words, w1_scales, w2_words, w2_scales, w3_words, w3_scales, offs, cen, pos1, pos2):
    xq = mxq(f64(xT)[:, unstriped(offs)], 0, "e4m3")
    h = unpack_fp4(w3_words, w3_scales).T @ xq
    g = unpack_fp4(w1_words, w1_scales).T @ xq
    gc = g[:, unstriped(cen)]
    s = unpack_fp4(w2_words, w2_scales).T @ xq
    sc = s[:, unstriped(cen)]
    return silu(h[:, unstriped(pos1)] * gc + sc) + silu(h[:, unstriped(pos2)] * gc + sc)

@@ -1,0 +1,148 @@
+from contextlib import ExitStack
+
+import concourse.mybir as mybir
+from concourse.masks import make_identity
+
+K, T, S, V, N = 512, 1024, 512, 256, 256
+FLOPS = 3 * 2 * K * N * S
+
+F32 = mybir.dt.float32
+BF16 = mybir.dt.bfloat16
+I32 = mybir.dt.int32
+U32 = mybir.dt.uint32
+U16 = mybir.dt.uint16
+U8 = mybir.dt.uint8
+FP8X4 = mybir.dt.float8_e4m3fn_x4
+FP4X4 = mybir.dt.float4_e2m1fn_x4
+MULT = mybir.AluOpType.mult
+ADD = mybir.AluOpType.add
+SILU = mybir.ActivationFunctionType.Silu
+
+P = 128
+H = S // 2
+
+
+def tile_picked_filmg_silu_e_kernel(tc, xT, w1_words, w1_scales, w2_words, w2_scales, w3_words, w3_scales, offs, cen, pos1, pos2, out):
+    nc = tc.nc
+    with ExitStack() as ctx:
+        keep = ctx.enter_context(tc.tile_pool(name="keep", bufs=1))
+        psum = ctx.enter_context(tc.psum_pool(name="psum", bufs=1))
+
+        offs_t = keep.tile([P, S // 16], U16, name="offs_t")
+        cen_t = keep.tile([P, V // 16], U16, name="cen_t")
+        pos_t = [keep.tile([P, V // 16], U16, name="pos_t%d" % d) for d in range(2)]
+        raw = [keep.tile([P, T], F32, name="raw%d" % j) for j in range(4)]
+        planes = xT.rearrange("(p j) t -> j p t", j=4)
+        nc.sync.dma_start(raw[0][:], planes[0])
+        nc.sync.dma_start(offs_t[:], offs)
+        nc.sync.dma_start(cen_t[:], cen)
+        nc.sync.dma_start(pos_t[0][:], pos1)
+        nc.sync.dma_start(pos_t[1][:], pos2)
+        for j in range(1, 4):
+            nc.sync.dma_start(raw[j][:], planes[j])
+        w_words = [keep.tile([P, 2 * N], U8, name="w_words%d" % i, align_bytes=64) for i in range(3)]
+        for i, w in enumerate((w1_words, w2_words, w3_words)):
+            nc.sync.dma_start(w_words[i][:].bitcast(I32), w[0].bitcast(I32))
+
+        w_scales = keep.tile([P, 3 * N], U8, name="w_scales", align_bytes=64)
+        nc.gpsimd.memset(w_scales[:].bitcast(I32), 0)
+        for i, sc in enumerate((w1_scales, w2_scales, w3_scales)):
+            nc.gpsimd.dma_start(w_scales[0:16, i * N:(i + 1) * N].bitcast(I32), sc[0].bitcast(I32))
+        warm = keep.tile([P, 8], F32, name="warm")
+        nc.vector.memset(warm[:, 0:1], 0.0)
+        nc.scalar.activation(warm[:, 4:5], warm[:, 0:1], SILU)
+        for q in range(1, 4):
+            nc.sync.dma_start(w_scales[32 * q:32 * q + 4, :].bitcast(I32), w_scales[4 * q:4 * q + 4, :].bitcast(I32))
+
+        ident = keep.tile([P, P], F32, name="ident")
+        nc.vector.memset(ident[:], 0.0)
+        make_identity(nc, ident[:], nomemset=True)
+
+        low = [keep.tile([P, 2, H], BF16, name="low%d" % a) for a in range(2)]
+        high = [keep.tile([P, 2, H], BF16, name="high%d" % a) for a in range(2)]
+        grouped = [keep.tile([P, H, 4], BF16, name="grouped%d" % a, align_bytes=64) for a in range(2)]
+        codes = keep.tile([P, S], U32, name="codes", align_bytes=64)
+        scales = keep.tile([P, S], U8, name="scales", align_bytes=64)
+
+        def half_list(a):
+            return offs_t[:, a * (H // 16):(a + 1) * (H // 16)]
+
+        for j in range(2):
+            for a in range(2):
+                nc.vector.tensor_copy(low[a][:, j, :], raw[j][:].indirect(half_list(a)))
+        for a in range(2):
+            nc.scalar.copy(grouped[a][:, :, 0:2], low[a][:].rearrange("p j w -> p w j"))
+        for j in range(2):
+            for a in range(2):
+                nc.vector.tensor_copy(high[a][:, j, :], raw[2 + j][:].indirect(half_list(a)))
+        nc.scalar.copy(grouped[0][:, :, 2:4], high[0][:].rearrange("p j w -> p w j"))
+        nc.vector.tensor_copy(grouped[1][:, :, 2:4], high[1][:].rearrange("p j w -> p w j"))
+        for a in range(2):
+            cols = slice(a * H, (a + 1) * H)
+            nc.vector.quantize_mx(out=codes[:, cols].bitcast(FP8X4), scales=scales[:, cols], in_=grouped[a][:].rearrange("p w j -> p (w j)"))
+
+        res = [[keep.tile([P, S], F32, name="res%d_%d" % (m, i)) for i in range(3)] for m in range(2)]
+
+        def product(m, i, cols, bank):
+            width = cols.stop - cols.start
+            acc = psum.tile([P, S], F32, name="acc", tag="bank%d" % bank)
+            nc.tensor.matmul_mx(
+                out=acc[:, 0:width],
+                lhsT=w_words[i][:, 2 * P * m:2 * P * (m + 1)].bitcast(FP4X4),
+                lhsT_scale=w_scales[:, i * N + P * m:i * N + P * (m + 1)],
+                rhs=codes[:, cols].bitcast(FP8X4),
+                rhs_scale=scales[:, cols],
+                start=True, stop=True)
+            return acc[:, 0:width]
+
+        first, second, whole = slice(0, H), slice(H, S), slice(0, S)
+        nc.scalar.copy(res[0][0][:, first], product(0, 0, first, 0))
+        nc.scalar.copy(res[0][0][:, second], product(0, 0, second, 1))
+        nc.scalar.copy(res[0][1][:, second], product(0, 1, second, 2))
+        nc.scalar.copy(res[0][1][:, first], product(0, 1, first, 0))
+        nc.scalar.copy(res[0][2][:], product(0, 2, whole, 3))
+        for i in range(3):
+            nc.scalar.copy(res[1][i][:], product(1, i, whole, 4 + i))
+
+        gc = [keep.tile([P, V], F32, name="gc%d" % m) for m in range(2)]
+        sc = [keep.tile([P, V], F32, name="sc%d" % m) for m in range(2)]
+        prod = [[keep.tile([P, V], F32, name="prod%d_%d" % (m, d)) for d in range(2)] for m in range(2)]
+
+        nc.vector.tensor_copy(gc[0][:], res[0][0][:].indirect(cen_t[:]))
+        nc.vector.tensor_copy(sc[0][:], res[0][1][:].indirect(cen_t[:]))
+        for d in range(2):
+            nc.vector.tensor_tensor(prod[0][d][:], res[0][2][:].indirect(pos_t[d][:]), gc[0][:], MULT)
+        pre = psum.tile([P, 2, V], F32, name="pre", tag="bank7")
+        for d in range(2):
+            for b in range(2):
+                blk = slice(b * P, (b + 1) * P)
+                nc.tensor.matmul(pre[:, d, blk], prod[0][d][:, blk], ident[:], start=True, stop=False, is_transpose=True)
+                nc.tensor.matmul(pre[:, d, blk], sc[0][:, blk], ident[:], start=False, stop=True, is_transpose=True)
+        act0 = keep.tile([P, 2, V], F32, name="act0")
+        nc.scalar.activation(act0[:], pre[:], SILU)
+        total = psum.tile([P, S], F32, name="total", tag="bank1")
+        for b in range(2):
+            blk = slice(b * P, (b + 1) * P)
+            for d in range(2):
+                nc.tensor.matmul(total[:, blk], act0[:, d, blk], ident[:], start=(d == 0), stop=(d == 1), is_transpose=True)
+        out0 = keep.tile([P, V], F32, name="out0")
+        nc.scalar.copy(out0[:], total[:, 0:V])
+        nc.sync.dma_start(out[0:P, :], out0[:])
+
+        halves = [slice(b * P, (b + 1) * P) for b in range(2)]
+        pre1 = [keep.tile([P, V], F32, name="pre1_%d" % d) for d in range(2)]
+        act1 = [keep.tile([P, V], F32, name="act1_%d" % d) for d in range(2)]
+        out1 = keep.tile([P, V], F32, name="out1")
+        nc.vector.tensor_copy(gc[1][:], res[1][0][:].indirect(cen_t[:]))
+        nc.vector.tensor_copy(sc[1][:], res[1][1][:].indirect(cen_t[:]))
+        nc.vector.tensor_tensor(prod[1][0][:], res[1][2][:].indirect(pos_t[0][:]), gc[1][:], MULT)
+        nc.vector.tensor_tensor(prod[1][1][:, halves[0]], res[1][2][:].indirect(pos_t[1][:, 0:8]), gc[1][:, halves[0]], MULT)
+        nc.vector.tensor_tensor(pre1[0][:], prod[1][0][:], sc[1][:], ADD)
+        nc.scalar.activation(act1[0][:], pre1[0][:], SILU)
+        nc.vector.tensor_tensor(prod[1][1][:, halves[1]], res[1][2][:].indirect(pos_t[1][:, 8:16]), gc[1][:, halves[1]], MULT)
+        for blk in halves:
+            nc.vector.tensor_tensor(pre1[1][:, blk], prod[1][1][:, blk], sc[1][:, blk], ADD)
+            nc.scalar.activation(act1[1][:, blk], pre1[1][:, blk], SILU)
+        for blk in halves:
+            nc.vector.tensor_tensor(out1[:, blk], act1[0][:, blk], act1[1][:, blk], ADD)
+            nc.sync.dma_start(out[P:2 * P, blk], out1[:, blk])

@@ -33,11 +33,11 @@ def tile_picked_filmg_silu_e_kernel(tc, xT, w1_words, w1_scales, w2_words, w2_sc
         pos_t = [keep.tile([P, V // 16], U16, name="pos_t%d" % d) for d in range(2)]
         raw = [keep.tile([P, T], F32, name="raw%d" % j) for j in range(4)]
         planes = xT.rearrange("(p j) t -> j p t", j=4)
+        staged = keep.tile([16, 3 * N], U8, name="staged")
+        for i, sc in enumerate((w1_scales, w2_scales, w3_scales)):
+            nc.scalar.dma_start(staged[:, i * N:(i + 1) * N].bitcast(I32), sc[0].bitcast(I32))
         nc.sync.dma_start(raw[0][:], planes[0])
         nc.sync.dma_start(offs_t[:], offs)
-        nc.sync.dma_start(cen_t[:], cen)
-        nc.sync.dma_start(pos_t[0][:], pos1)
-        nc.sync.dma_start(pos_t[1][:], pos2)
         for j in range(1, 4):
             nc.sync.dma_start(raw[j][:], planes[j])
         w_words = [keep.tile([P, 2 * N], U8, name="w_words%d" % i, align_bytes=64) for i in range(3)]
@@ -46,40 +46,49 @@ def tile_picked_filmg_silu_e_kernel(tc, xT, w1_words, w1_scales, w2_words, w2_sc
 
         w_scales = keep.tile([P, 3 * N], U8, name="w_scales", align_bytes=64)
         nc.gpsimd.memset(w_scales[:].bitcast(I32), 0)
-        for i, sc in enumerate((w1_scales, w2_scales, w3_scales)):
-            nc.gpsimd.dma_start(w_scales[0:16, i * N:(i + 1) * N].bitcast(I32), sc[0].bitcast(I32))
+        nc.gpsimd.tensor_copy(w_scales[0:4, :].bitcast(I32), staged[0:4, :].bitcast(I32))
+        for q in range(1, 4):
+            nc.scalar.dma_start(w_scales[32 * q:32 * q + 4, :].bitcast(I32), staged[4 * q:4 * q + 4, :].bitcast(I32))
+        nc.sync.dma_start(cen_t[:], cen)
+        nc.sync.dma_start(pos_t[0][:], pos1)
+        nc.sync.dma_start(pos_t[1][:], pos2)
         warm = keep.tile([P, 8], F32, name="warm")
         nc.vector.memset(warm[:, 0:1], 0.0)
         nc.scalar.activation(warm[:, 4:5], warm[:, 0:1], SILU)
-        for q in range(1, 4):
-            nc.sync.dma_start(w_scales[32 * q:32 * q + 4, :].bitcast(I32), w_scales[4 * q:4 * q + 4, :].bitcast(I32))
 
         ident = keep.tile([P, P], F32, name="ident")
         nc.vector.memset(ident[:], 0.0)
         make_identity(nc, ident[:], nomemset=True)
 
+        Q = S // 4
         low = [keep.tile([P, 2, H], BF16, name="low%d" % a) for a in range(2)]
-        high = [keep.tile([P, 2, H], BF16, name="high%d" % a) for a in range(2)]
-        grouped = [keep.tile([P, H, 4], BF16, name="grouped%d" % a, align_bytes=64) for a in range(2)]
+        high = [keep.tile([P, 2, Q], BF16, name="high%d" % a) for a in range(3)]
+        front = keep.tile([P, H, 4], BF16, name="front", align_bytes=64)
+        third = keep.tile([P, Q, 4], BF16, name="third", align_bytes=64)
+        last = keep.tile([P, Q, 4], BF16, name="last", align_bytes=64)
+        quarter = [front[:, 0:Q, :], front[:, Q:H, :], third[:], last[:]]
         codes = keep.tile([P, S], U32, name="codes", align_bytes=64)
         scales = keep.tile([P, S], U8, name="scales", align_bytes=64)
 
-        def half_list(a):
-            return offs_t[:, a * (H // 16):(a + 1) * (H // 16)]
+        def entries(first, count):
+            return offs_t[:, first // 16:(first + count) // 16]
 
         for j in range(2):
             for a in range(2):
-                nc.vector.tensor_copy(low[a][:, j, :], raw[j][:].indirect(half_list(a)))
-        for a in range(2):
-            nc.scalar.copy(grouped[a][:, :, 0:2], low[a][:].rearrange("p j w -> p w j"))
+                nc.vector.tensor_copy(low[a][:, j, :], raw[j][:].indirect(entries(a * H, H)))
+        nc.scalar.copy(front[:, :, 0:2], low[0][:].rearrange("p j w -> p w j"))
+        for b in range(2):
+            nc.scalar.copy(quarter[2 + b][:, :, 0:2], low[1][:, :, b * Q:(b + 1) * Q].rearrange("p j w -> p w j"))
         for j in range(2):
-            for a in range(2):
-                nc.vector.tensor_copy(high[a][:, j, :], raw[2 + j][:].indirect(half_list(a)))
-        nc.scalar.copy(grouped[0][:, :, 2:4], high[0][:].rearrange("p j w -> p w j"))
-        nc.vector.tensor_copy(grouped[1][:, :, 2:4], high[1][:].rearrange("p j w -> p w j"))
-        for a in range(2):
-            cols = slice(a * H, (a + 1) * H)
-            nc.vector.quantize_mx(out=codes[:, cols].bitcast(FP8X4), scales=scales[:, cols], in_=grouped[a][:].rearrange("p w j -> p (w j)"))
+            for a in range(3):
+                nc.vector.tensor_copy(high[a][:, j, :], raw[2 + j][:].indirect(entries(a * Q, Q)))
+            nc.vector.tensor_copy(last[:, :, 2 + j], raw[2 + j][:].indirect(entries(3 * Q, Q)))
+        for a in range(3):
+            nc.scalar.copy(quarter[a][:, :, 2:4], high[a][:].rearrange("p j w -> p w j"))
+        first, second, whole = slice(0, H), slice(H, S), slice(0, S)
+        third_cols, last_cols = slice(H, H + Q), slice(H + Q, S)
+        for grouped, cols in ((front, first), (last, last_cols), (third, third_cols)):
+            nc.vector.quantize_mx(out=codes[:, cols].bitcast(FP8X4), scales=scales[:, cols], in_=grouped[:].rearrange("p w j -> p (w j)"))
 
         res = [[keep.tile([P, S], F32, name="res%d_%d" % (m, i)) for i in range(3)] for m in range(2)]
 
@@ -95,14 +104,15 @@ def tile_picked_filmg_silu_e_kernel(tc, xT, w1_words, w1_scales, w2_words, w2_sc
                 start=True, stop=True)
             return acc[:, 0:width]
 
-        first, second, whole = slice(0, H), slice(H, S), slice(0, S)
-        nc.scalar.copy(res[0][0][:, first], product(0, 0, first, 0))
-        nc.scalar.copy(res[0][0][:, second], product(0, 0, second, 1))
-        nc.scalar.copy(res[0][1][:, second], product(0, 1, second, 2))
+        nc.vector.tensor_copy(res[0][0][:, first], product(0, 0, first, 0))
+        nc.scalar.copy(res[0][0][:, last_cols], product(0, 0, last_cols, 1))
+        nc.scalar.copy(res[0][0][:, third_cols], product(0, 0, third_cols, 2))
+        nc.scalar.copy(res[0][1][:, second], product(0, 1, second, 3))
         nc.scalar.copy(res[0][1][:, first], product(0, 1, first, 0))
-        nc.scalar.copy(res[0][2][:], product(0, 2, whole, 3))
+        nc.scalar.copy(res[0][2][:, second], product(0, 2, second, 4))
+        nc.scalar.copy(res[0][2][:, first], product(0, 2, first, 1))
         for i in range(3):
-            nc.scalar.copy(res[1][i][:], product(1, i, whole, 4 + i))
+            nc.scalar.copy(res[1][i][:], product(1, i, whole, 5 + i))
 
         gc = [keep.tile([P, V], F32, name="gc%d" % m) for m in range(2)]
         sc = [keep.tile([P, V], F32, name="sc%d" % m) for m in range(2)]
@@ -112,15 +122,15 @@ def tile_picked_filmg_silu_e_kernel(tc, xT, w1_words, w1_scales, w2_words, w2_sc
         nc.vector.tensor_copy(sc[0][:], res[0][1][:].indirect(cen_t[:]))
         for d in range(2):
             nc.vector.tensor_tensor(prod[0][d][:], res[0][2][:].indirect(pos_t[d][:]), gc[0][:], MULT)
-        pre = psum.tile([P, 2, V], F32, name="pre", tag="bank7")
+        act0 = keep.tile([P, 2, V], F32, name="act0")
         for d in range(2):
+            pre = psum.tile([P, S], F32, name="pre", tag="bank%d" % (2 * d))
             for b in range(2):
                 blk = slice(b * P, (b + 1) * P)
-                nc.tensor.matmul(pre[:, d, blk], prod[0][d][:, blk], ident[:], start=True, stop=False, is_transpose=True)
-                nc.tensor.matmul(pre[:, d, blk], sc[0][:, blk], ident[:], start=False, stop=True, is_transpose=True)
-        act0 = keep.tile([P, 2, V], F32, name="act0")
-        nc.scalar.activation(act0[:], pre[:], SILU)
-        total = psum.tile([P, S], F32, name="total", tag="bank1")
+                nc.tensor.matmul(pre[:, blk], sc[0][:, blk], ident[:], start=True, stop=False, is_transpose=True)
+                nc.tensor.matmul(pre[:, blk], prod[0][d][:, blk], ident[:], start=False, stop=True, is_transpose=True)
+            nc.scalar.activation(act0[:, d, :], pre[:, 0:V], SILU)
+        total = psum.tile([P, S], F32, name="total", tag="bank3")
         for b in range(2):
             blk = slice(b * P, (b + 1) * P)
             for d in range(2):
@@ -130,19 +140,26 @@ def tile_picked_filmg_silu_e_kernel(tc, xT, w1_words, w1_scales, w2_words, w2_sc
         nc.sync.dma_start(out[0:P, :], out0[:])
 
         halves = [slice(b * P, (b + 1) * P) for b in range(2)]
-        pre1 = [keep.tile([P, V], F32, name="pre1_%d" % d) for d in range(2)]
+        pre1 = prod[1][0]
         act1 = [keep.tile([P, V], F32, name="act1_%d" % d) for d in range(2)]
         out1 = keep.tile([P, V], F32, name="out1")
         nc.vector.tensor_copy(gc[1][:], res[1][0][:].indirect(cen_t[:]))
         nc.vector.tensor_copy(sc[1][:], res[1][1][:].indirect(cen_t[:]))
         nc.vector.tensor_tensor(prod[1][0][:], res[1][2][:].indirect(pos_t[0][:]), gc[1][:], MULT)
-        nc.vector.tensor_tensor(prod[1][1][:, halves[0]], res[1][2][:].indirect(pos_t[1][:, 0:8]), gc[1][:, halves[0]], MULT)
-        nc.vector.tensor_tensor(pre1[0][:], prod[1][0][:], sc[1][:], ADD)
-        nc.scalar.activation(act1[0][:], pre1[0][:], SILU)
-        nc.vector.tensor_tensor(prod[1][1][:, halves[1]], res[1][2][:].indirect(pos_t[1][:, 8:16]), gc[1][:, halves[1]], MULT)
+        turned = [psum.tile([P, S], F32, name="turned", tag="bank%d" % (2 * b)) for b in range(2)]
+        back = [psum.tile([P, S], F32, name="back", tag="bank%d" % (4 + b)) for b in range(2)]
+        for b, blk in enumerate(halves):
+            nc.tensor.matmul(turned[b][:, 0:P], sc[1][:, blk], ident[:], start=True, stop=False, is_transpose=True)
+        for b, blk in enumerate(halves):
+            nc.tensor.matmul(turned[b][:, 0:P], prod[1][0][:, blk], ident[:], start=False, stop=True, is_transpose=True)
+        for b, blk in enumerate(halves):
+            nc.scalar.activation(act1[0][:, blk], turned[b][:, 0:P], SILU)
+            nc.tensor.transpose(back[b][:, 0:P], act1[0][:, blk], ident[:])
+        for b, blk in enumerate(halves):
+            nc.vector.tensor_tensor(prod[1][1][:, blk], res[1][2][:].indirect(pos_t[1][:, 8 * b:8 * b + 8]), gc[1][:, blk], MULT)
         for blk in halves:
-            nc.vector.tensor_tensor(pre1[1][:, blk], prod[1][1][:, blk], sc[1][:, blk], ADD)
-            nc.scalar.activation(act1[1][:, blk], pre1[1][:, blk], SILU)
-        for blk in halves:
-            nc.vector.tensor_tensor(out1[:, blk], act1[0][:, blk], act1[1][:, blk], ADD)
+            nc.vector.tensor_tensor(pre1[:, blk], prod[1][1][:, blk], sc[1][:, blk], ADD)
+            nc.scalar.activation(act1[1][:, blk], pre1[:, blk], SILU)
+        for b, blk in enumerate(halves):
+            nc.vector.tensor_tensor(out1[:, blk], act1[1][:, blk], back[b][:, 0:P], ADD)
             nc.sync.dma_start(out[P:2 * P, blk], out1[:, blk])

@@ -122,44 +122,54 @@ def tile_picked_filmg_silu_e_kernel(tc, xT, w1_words, w1_scales, w2_words, w2_sc
         nc.vector.tensor_copy(sc[0][:], res[0][1][:].indirect(cen_t[:]))
         for d in range(2):
             nc.vector.tensor_tensor(prod[0][d][:], res[0][2][:].indirect(pos_t[d][:]), gc[0][:], MULT)
+        halves = [slice(b * P, (b + 1) * P) for b in range(2)]
+
+        def bank(tag):
+            return psum.tile([P, S], F32, name="acc", tag="bank%d" % tag)
+
+        def turn(acc, block, start, stop):
+            nc.tensor.matmul(acc, block, ident[:], start=start, stop=stop, is_transpose=True)
+
         act0 = keep.tile([P, 2, V], F32, name="act0")
-        for d in range(2):
-            pre = psum.tile([P, S], F32, name="pre", tag="bank%d" % (2 * d))
-            for b in range(2):
-                blk = slice(b * P, (b + 1) * P)
-                nc.tensor.matmul(pre[:, blk], sc[0][:, blk], ident[:], start=True, stop=False, is_transpose=True)
-                nc.tensor.matmul(pre[:, blk], prod[0][d][:, blk], ident[:], start=False, stop=True, is_transpose=True)
-            nc.scalar.activation(act0[:, d, :], pre[:, 0:V], SILU)
-        total = psum.tile([P, S], F32, name="total", tag="bank3")
-        for b in range(2):
-            blk = slice(b * P, (b + 1) * P)
-            for d in range(2):
-                nc.tensor.matmul(total[:, blk], act0[:, d, blk], ident[:], start=(d == 0), stop=(d == 1), is_transpose=True)
         out0 = keep.tile([P, V], F32, name="out0")
-        nc.scalar.copy(out0[:], total[:, 0:V])
+        pre = bank(0)
+        for blk in halves:
+            turn(pre[:, blk], sc[0][:, blk], True, False)
+            turn(pre[:, blk], prod[0][0][:, blk], False, True)
+        nc.scalar.activation(act0[:, 0, :], pre[:, 0:V], SILU)
+        total = [bank(3 + b) for b in range(2)]
+        for b, blk in enumerate(halves):
+            pre = bank(1 + b)
+            turn(pre[:, 0:P], sc[0][:, blk], True, False)
+            turn(pre[:, 0:P], prod[0][1][:, blk], False, True)
+            nc.scalar.activation(act0[:, 1, blk], pre[:, 0:P], SILU)
+        for b, blk in enumerate(halves):
+            turn(total[b][:, 0:P], act0[:, 0, blk], True, False)
+        for b, blk in enumerate(halves):
+            turn(total[b][:, 0:P], act0[:, 1, blk], False, True)
+            nc.scalar.copy(out0[:, blk], total[b][:, 0:P])
         nc.sync.dma_start(out[0:P, :], out0[:])
 
-        halves = [slice(b * P, (b + 1) * P) for b in range(2)]
-        pre1 = prod[1][0]
         act1 = [keep.tile([P, V], F32, name="act1_%d" % d) for d in range(2)]
         out1 = keep.tile([P, V], F32, name="out1")
         nc.vector.tensor_copy(gc[1][:], res[1][0][:].indirect(cen_t[:]))
         nc.vector.tensor_copy(sc[1][:], res[1][1][:].indirect(cen_t[:]))
-        nc.vector.tensor_tensor(prod[1][0][:], res[1][2][:].indirect(pos_t[0][:]), gc[1][:], MULT)
-        turned = [psum.tile([P, S], F32, name="turned", tag="bank%d" % (2 * b)) for b in range(2)]
-        back = [psum.tile([P, S], F32, name="back", tag="bank%d" % (4 + b)) for b in range(2)]
         for b, blk in enumerate(halves):
-            nc.tensor.matmul(turned[b][:, 0:P], sc[1][:, blk], ident[:], start=True, stop=False, is_transpose=True)
+            nc.vector.tensor_tensor(prod[1][0][:, blk], res[1][2][:].indirect(pos_t[0][:, 8 * b:8 * b + 8]), gc[1][:, blk], MULT)
+        back = []
         for b, blk in enumerate(halves):
-            nc.tensor.matmul(turned[b][:, 0:P], prod[1][0][:, blk], ident[:], start=False, stop=True, is_transpose=True)
+            turned = bank(1 + b)
+            turn(turned[:, 0:P], sc[1][:, blk], True, False)
+            turn(turned[:, 0:P], prod[1][0][:, blk], False, True)
+            nc.scalar.activation(act1[0][:, blk], turned[:, 0:P], SILU)
         for b, blk in enumerate(halves):
-            nc.scalar.activation(act1[0][:, blk], turned[b][:, 0:P], SILU)
-            nc.tensor.transpose(back[b][:, 0:P], act1[0][:, blk], ident[:])
+            back.append(bank(5 * b))
+            turn(back[b][:, 0:P], act1[0][:, blk], True, True)
         for b, blk in enumerate(halves):
             nc.vector.tensor_tensor(prod[1][1][:, blk], res[1][2][:].indirect(pos_t[1][:, 8 * b:8 * b + 8]), gc[1][:, blk], MULT)
-        for blk in halves:
-            nc.vector.tensor_tensor(pre1[:, blk], prod[1][1][:, blk], sc[1][:, blk], ADD)
-            nc.scalar.activation(act1[1][:, blk], pre1[:, blk], SILU)
+        for blk, spare in zip(halves, (prod[1][0][:, halves[1]], prod[1][1][:, halves[0]])):
+            nc.vector.tensor_tensor(spare, prod[1][1][:, blk], sc[1][:, blk], ADD)
+            nc.scalar.activation(act1[1][:, blk], spare, SILU)
         for b, blk in enumerate(halves):
             nc.vector.tensor_tensor(out1[:, blk], act1[1][:, blk], back[b][:, 0:P], ADD)
             nc.sync.dma_start(out[P:2 * P, blk], out1[:, blk])

@@ -33,22 +33,20 @@ def tile_picked_filmg_silu_e_kernel(tc, xT, w1_words, w1_scales, w2_words, w2_sc
         pos_t = [keep.tile([P, V // 16], U16, name="pos_t%d" % d) for d in range(2)]
         raw = [keep.tile([P, T], F32, name="raw%d" % j) for j in range(4)]
         planes = xT.rearrange("(p j) t -> j p t", j=4)
-        staged = keep.tile([16, 3 * N], U8, name="staged")
-        for i, sc in enumerate((w1_scales, w2_scales, w3_scales)):
-            nc.scalar.dma_start(staged[:, i * N:(i + 1) * N].bitcast(I32), sc[0].bitcast(I32))
+        w_scales = keep.tile([P, 3 * N], U8, name="w_scales", align_bytes=64)
+        nc.vector.memset(w_scales[:].bitcast(I32), 0)
         nc.sync.dma_start(raw[0][:], planes[0])
         nc.sync.dma_start(offs_t[:], offs)
+        for i, sc in enumerate((w1_scales, w2_scales, w3_scales)):
+            nc.sync.dma_start(w_scales[0:16, i * N:(i + 1) * N].bitcast(I32), sc[0].bitcast(I32))
         for j in range(1, 4):
             nc.sync.dma_start(raw[j][:], planes[j])
         w_words = [keep.tile([P, 2 * N], U8, name="w_words%d" % i, align_bytes=64) for i in range(3)]
         for i, w in enumerate((w1_words, w2_words, w3_words)):
             nc.sync.dma_start(w_words[i][:].bitcast(I32), w[0].bitcast(I32))
 
-        w_scales = keep.tile([P, 3 * N], U8, name="w_scales", align_bytes=64)
-        nc.gpsimd.memset(w_scales[:].bitcast(I32), 0)
-        nc.gpsimd.tensor_copy(w_scales[0:4, :].bitcast(I32), staged[0:4, :].bitcast(I32))
         for q in range(1, 4):
-            nc.scalar.dma_start(w_scales[32 * q:32 * q + 4, :].bitcast(I32), staged[4 * q:4 * q + 4, :].bitcast(I32))
+            nc.sync.dma_start(w_scales[32 * q:32 * q + 4, :].bitcast(I32), w_scales[4 * q:4 * q + 4, :].bitcast(I32))
         nc.sync.dma_start(cen_t[:], cen)
         nc.sync.dma_start(pos_t[0][:], pos1)
         nc.sync.dma_start(pos_t[1][:], pos2)
@@ -61,8 +59,8 @@ def tile_picked_filmg_silu_e_kernel(tc, xT, w1_words, w1_scales, w2_words, w2_sc
         make_identity(nc, ident[:], nomemset=True)
 
         Q = S // 4
-        low = [keep.tile([P, 2, H], BF16, name="low%d" % a) for a in range(2)]
-        high = [keep.tile([P, 2, Q], BF16, name="high%d" % a) for a in range(3)]
+        low = keep.tile([P, 2, S], BF16, name="low")
+        high = keep.tile([P, 2, 3 * Q], BF16, name="high")
         front = keep.tile([P, H, 4], BF16, name="front", align_bytes=64)
         third = keep.tile([P, Q, 4], BF16, name="third", align_bytes=64)
         last = keep.tile([P, Q, 4], BF16, name="last", align_bytes=64)
@@ -73,22 +71,23 @@ def tile_picked_filmg_silu_e_kernel(tc, xT, w1_words, w1_scales, w2_words, w2_sc
         def entries(first, count):
             return offs_t[:, first // 16:(first + count) // 16]
 
-        for j in range(2):
-            for a in range(2):
-                nc.vector.tensor_copy(low[a][:, j, :], raw[j][:].indirect(entries(a * H, H)))
-        nc.scalar.copy(front[:, :, 0:2], low[0][:].rearrange("p j w -> p w j"))
-        for b in range(2):
-            nc.scalar.copy(quarter[2 + b][:, :, 0:2], low[1][:, :, b * Q:(b + 1) * Q].rearrange("p j w -> p w j"))
-        for j in range(2):
-            for a in range(3):
-                nc.vector.tensor_copy(high[a][:, j, :], raw[2 + j][:].indirect(entries(a * Q, Q)))
-            nc.vector.tensor_copy(last[:, :, 2 + j], raw[2 + j][:].indirect(entries(3 * Q, Q)))
+        nc.vector.tensor_copy(low[:, 0, :], raw[0][:].indirect(offs_t[:]))
+        for a in range(2):
+            nc.vector.tensor_copy(low[:, 1, a * H:(a + 1) * H], raw[1][:].indirect(entries(a * H, H)))
+        nc.scalar.copy(front[:, :, 0:2], low[:, :, 0:H].rearrange("p j w -> p w j"))
+        for a in range(2, 4):
+            nc.scalar.copy(quarter[a][:, :, 0:2], low[:, :, a * Q:(a + 1) * Q].rearrange("p j w -> p w j"))
+        nc.vector.tensor_copy(high[:, 0, :], raw[2][:].indirect(entries(0, 3 * Q)))
+        nc.vector.tensor_copy(last[:, :, 2], raw[2][:].indirect(entries(3 * Q, Q)))
         for a in range(3):
-            nc.scalar.copy(quarter[a][:, :, 2:4], high[a][:].rearrange("p j w -> p w j"))
+            nc.vector.tensor_copy(high[:, 1, a * Q:(a + 1) * Q], raw[3][:].indirect(entries(a * Q, Q)))
+            nc.scalar.copy(quarter[a][:, :, 2:4], high[:, :, a * Q:(a + 1) * Q].rearrange("p j w -> p w j"))
+        nc.vector.tensor_copy(last[:, :, 3], raw[3][:].indirect(entries(3 * Q, Q)))
         first, second, whole = slice(0, H), slice(H, S), slice(0, S)
-        third_cols, last_cols = slice(H, H + Q), slice(H + Q, S)
-        for grouped, cols in ((front, first), (last, last_cols), (third, third_cols)):
-            nc.vector.quantize_mx(out=codes[:, cols].bitcast(FP8X4), scales=scales[:, cols], in_=grouped[:].rearrange("p w j -> p (w j)"))
+        cols_of = [slice(a * Q, (a + 1) * Q) for a in range(4)]
+        order = (0, 1, 3, 2)
+        for a in order:
+            nc.vector.quantize_mx(out=codes[:, cols_of[a]].bitcast(FP8X4), scales=scales[:, cols_of[a]], in_=quarter[a].rearrange("p w j -> p (w j)"))
 
         res = [[keep.tile([P, S], F32, name="res%d_%d" % (m, i)) for i in range(3)] for m in range(2)]
 
@@ -104,15 +103,15 @@ def tile_picked_filmg_silu_e_kernel(tc, xT, w1_words, w1_scales, w2_words, w2_sc
                 start=True, stop=True)
             return acc[:, 0:width]
 
-        nc.vector.tensor_copy(res[0][0][:, first], product(0, 0, first, 0))
-        nc.scalar.copy(res[0][0][:, last_cols], product(0, 0, last_cols, 1))
-        nc.scalar.copy(res[0][0][:, third_cols], product(0, 0, third_cols, 2))
-        nc.scalar.copy(res[0][1][:, second], product(0, 1, second, 3))
+        for b, a in enumerate(order[:3]):
+            nc.vector.tensor_copy(res[0][0][:, cols_of[a]], product(0, 0, cols_of[a], b))
+        nc.scalar.copy(res[0][0][:, cols_of[order[3]]], product(0, 0, cols_of[order[3]], 3))
+        nc.scalar.copy(res[0][1][:, second], product(0, 1, second, 4))
         nc.scalar.copy(res[0][1][:, first], product(0, 1, first, 0))
-        nc.scalar.copy(res[0][2][:, second], product(0, 2, second, 4))
+        nc.scalar.copy(res[0][2][:, second], product(0, 2, second, 5))
         nc.scalar.copy(res[0][2][:, first], product(0, 2, first, 1))
-        for i in range(3):
-            nc.scalar.copy(res[1][i][:], product(1, i, whole, 5 + i))
+        for i, b in enumerate((6, 7, 2)):
+            nc.scalar.copy(res[1][i][:], product(1, i, whole, b))
 
         gc = [keep.tile([P, V], F32, name="gc%d" % m) for m in range(2)]
         sc = [keep.tile([P, V], F32, name="sc%d" % m) for m in range(2)]
@@ -132,17 +131,15 @@ def tile_picked_filmg_silu_e_kernel(tc, xT, w1_words, w1_scales, w2_words, w2_sc
 
         act0 = keep.tile([P, 2, V], F32, name="act0")
         out0 = keep.tile([P, V], F32, name="out0")
-        pre = bank(0)
-        for blk in halves:
-            turn(pre[:, blk], sc[0][:, blk], True, False)
-            turn(pre[:, blk], prod[0][0][:, blk], False, True)
-        nc.scalar.activation(act0[:, 0, :], pre[:, 0:V], SILU)
-        total = [bank(3 + b) for b in range(2)]
-        for b, blk in enumerate(halves):
-            pre = bank(1 + b)
-            turn(pre[:, 0:P], sc[0][:, blk], True, False)
-            turn(pre[:, 0:P], prod[0][1][:, blk], False, True)
-            nc.scalar.activation(act0[:, 1, blk], pre[:, 0:P], SILU)
+        pre = [[bank(t) for t in pair] for pair in ((3, 4), (0, 5))]
+        for d in range(2):
+            for b, blk in enumerate(halves):
+                turn(pre[d][b][:, 0:P], sc[0][:, blk], True, False)
+        for d in range(2):
+            for b, blk in enumerate(halves):
+                turn(pre[d][b][:, 0:P], prod[0][d][:, blk], False, True)
+                nc.scalar.activation(act0[:, d, blk], pre[d][b][:, 0:P], SILU)
+        total = [bank(t) for t in (1, 6)]
         for b, blk in enumerate(halves):
             turn(total[b][:, 0:P], act0[:, 0, blk], True, False)
         for b, blk in enumerate(halves):
@@ -158,12 +155,12 @@ def tile_picked_filmg_silu_e_kernel(tc, xT, w1_words, w1_scales, w2_words, w2_sc
             nc.vector.tensor_tensor(prod[1][0][:, blk], res[1][2][:].indirect(pos_t[0][:, 8 * b:8 * b + 8]), gc[1][:, blk], MULT)
         back = []
         for b, blk in enumerate(halves):
-            turned = bank(1 + b)
+            turned = bank((7, 2)[b])
             turn(turned[:, 0:P], sc[1][:, blk], True, False)
             turn(turned[:, 0:P], prod[1][0][:, blk], False, True)
             nc.scalar.activation(act1[0][:, blk], turned[:, 0:P], SILU)
         for b, blk in enumerate(halves):
-            back.append(bank(5 * b))
+            back.append(bank(3 + b))
             turn(back[b][:, 0:P], act1[0][:, blk], True, True)
         for b, blk in enumerate(halves):
             nc.vector.tensor_tensor(prod[1][1][:, blk], res[1][2][:].indirect(pos_t[1][:, 8 * b:8 * b + 8]), gc[1][:, blk], MULT)

@@ -16,6 +16,7 @@ FP8X4 = mybir.dt.float8_e4m3fn_x4
 FP4X4 = mybir.dt.float4_e2m1fn_x4
 MULT = mybir.AluOpType.mult
 ADD = mybir.AluOpType.add
+COPY = mybir.ActivationFunctionType.Copy
 SILU = mybir.ActivationFunctionType.Silu
 
 P = 128
@@ -37,10 +38,11 @@ def tile_picked_filmg_silu_e_kernel(tc, xT, w1_words, w1_scales, w2_words, w2_sc
         nc.vector.memset(w_scales[:].bitcast(I32), 0)
         nc.sync.dma_start(raw[0][:], planes[0])
         nc.sync.dma_start(offs_t[:], offs)
+        for j in (1, 2):
+            nc.sync.dma_start(raw[j][:], planes[j])
         for i, sc in enumerate((w1_scales, w2_scales, w3_scales)):
             nc.sync.dma_start(w_scales[0:16, i * N:(i + 1) * N].bitcast(I32), sc[0].bitcast(I32))
-        for j in range(1, 4):
-            nc.sync.dma_start(raw[j][:], planes[j])
+        nc.sync.dma_start(raw[3][:], planes[3])
         w_words = [keep.tile([P, 2 * N], U8, name="w_words%d" % i, align_bytes=64) for i in range(3)]
         for i, w in enumerate((w1_words, w2_words, w3_words)):
             nc.sync.dma_start(w_words[i][:].bitcast(I32), w[0].bitcast(I32))
@@ -71,7 +73,10 @@ def tile_picked_filmg_silu_e_kernel(tc, xT, w1_words, w1_scales, w2_words, w2_sc
         def entries(first, count):
             return offs_t[:, first // 16:(first + count) // 16]
 
-        nc.vector.tensor_copy(low[:, 0, :], raw[0][:].indirect(offs_t[:]))
+        rounded = keep.tile([P, T], BF16, name="rounded")
+        nc.scalar.copy(rounded[:], raw[0][:])
+        nc.scalar.activation(low[:, 0, 3 * Q:S], rounded[:].indirect(entries(3 * Q, Q)), COPY)
+        nc.vector.tensor_copy(low[:, 0, 0:3 * Q], raw[0][:].indirect(entries(0, 3 * Q)))
         for a in range(2):
             nc.vector.tensor_copy(low[:, 1, a * H:(a + 1) * H], raw[1][:].indirect(entries(a * H, H)))
         nc.scalar.copy(front[:, :, 0:2], low[:, :, 0:H].rearrange("p j w -> p w j"))
@@ -106,22 +111,27 @@ def tile_picked_filmg_silu_e_kernel(tc, xT, w1_words, w1_scales, w2_words, w2_sc
         for b, a in enumerate(order[:3]):
             nc.vector.tensor_copy(res[0][0][:, cols_of[a]], product(0, 0, cols_of[a], b))
         nc.scalar.copy(res[0][0][:, cols_of[order[3]]], product(0, 0, cols_of[order[3]], 3))
-        nc.scalar.copy(res[0][1][:, second], product(0, 1, second, 4))
-        nc.scalar.copy(res[0][1][:, first], product(0, 1, first, 0))
-        nc.scalar.copy(res[0][2][:, second], product(0, 2, second, 5))
-        nc.scalar.copy(res[0][2][:, first], product(0, 2, first, 1))
-        for i, b in enumerate((6, 7, 2)):
+        nc.scalar.copy(res[0][2][:, second], product(0, 2, second, 4))
+        nc.scalar.copy(res[0][2][:, first], product(0, 2, first, 0))
+        nc.scalar.copy(res[0][1][:], product(0, 1, whole, 1))
+        for i, b in enumerate((2, 3, 4)):
             nc.scalar.copy(res[1][i][:], product(1, i, whole, b))
 
         gc = [keep.tile([P, V], F32, name="gc%d" % m) for m in range(2)]
         sc = [keep.tile([P, V], F32, name="sc%d" % m) for m in range(2)]
         prod = [[keep.tile([P, V], F32, name="prod%d_%d" % (m, d)) for d in range(2)] for m in range(2)]
 
-        nc.vector.tensor_copy(gc[0][:], res[0][0][:].indirect(cen_t[:]))
-        nc.vector.tensor_copy(sc[0][:], res[0][1][:].indirect(cen_t[:]))
-        for d in range(2):
-            nc.vector.tensor_tensor(prod[0][d][:], res[0][2][:].indirect(pos_t[d][:]), gc[0][:], MULT)
         halves = [slice(b * P, (b + 1) * P) for b in range(2)]
+
+        def places(lst, blk):
+            return lst[:, blk.start // 16:blk.stop // 16]
+
+        for blk in halves:
+            nc.vector.tensor_copy(gc[0][:, blk], res[0][0][:].indirect(places(cen_t, blk)))
+        for blk in halves:
+            nc.vector.tensor_tensor(prod[0][0][:, blk], res[0][2][:].indirect(places(pos_t[0], blk)), gc[0][:, blk], MULT)
+        nc.vector.tensor_tensor(prod[0][1][:], res[0][2][:].indirect(pos_t[1][:]), gc[0][:], MULT)
+        nc.vector.tensor_copy(sc[0][:], res[0][1][:].indirect(cen_t[:]))
 
         def bank(tag):
             return psum.tile([P, S], F32, name="acc", tag="bank%d" % tag)
@@ -131,42 +141,46 @@ def tile_picked_filmg_silu_e_kernel(tc, xT, w1_words, w1_scales, w2_words, w2_sc
 
         act0 = keep.tile([P, 2, V], F32, name="act0")
         out0 = keep.tile([P, V], F32, name="out0")
-        pre = [[bank(t) for t in pair] for pair in ((3, 4), (0, 5))]
-        for d in range(2):
-            for b, blk in enumerate(halves):
-                turn(pre[d][b][:, 0:P], sc[0][:, blk], True, False)
-        for d in range(2):
-            for b, blk in enumerate(halves):
-                turn(pre[d][b][:, 0:P], prod[0][d][:, blk], False, True)
-                nc.scalar.activation(act0[:, d, blk], pre[d][b][:, 0:P], SILU)
-        total = [bank(t) for t in (1, 6)]
-        for b, blk in enumerate(halves):
-            turn(total[b][:, 0:P], act0[:, 0, blk], True, False)
-        for b, blk in enumerate(halves):
-            turn(total[b][:, 0:P], act0[:, 1, blk], False, True)
-            nc.scalar.copy(out0[:, blk], total[b][:, 0:P])
-        nc.sync.dma_start(out[0:P, :], out0[:])
+        for d, tag in enumerate((5, 6)):
+            pre = bank(tag)
+            for blk in halves:
+                turn(pre[:, blk], prod[0][d][:, blk], True, False)
+                turn(pre[:, blk], sc[0][:, blk], False, True)
+            nc.scalar.activation(act0[:, d, :], pre[:, 0:V], SILU)
+        total = bank(0)
+        for blk in halves:
+            for d in range(2):
+                turn(total[:, blk], act0[:, d, blk], d == 0, d == 1)
 
-        act1 = [keep.tile([P, V], F32, name="act1_%d" % d) for d in range(2)]
-        out1 = keep.tile([P, V], F32, name="out1")
+        left, right = halves
+
+        out1 = [keep.tile([P, P], F32, name="out1_%d" % b) for b in range(2)]
+        act1 = [keep.tile([P, P], F32, name="act1_%d" % d) for d in range(2)]
+        pre1 = [keep.tile([P, P], F32, name="pre1_%d" % d) for d in range(2)]
+        reused = keep.tile([P, V], F32, name="reused")
+        prod_left = [prod[1][0][:, left], reused[:, P // 2:P // 2 + P]]
         nc.vector.tensor_copy(gc[1][:], res[1][0][:].indirect(cen_t[:]))
-        nc.vector.tensor_copy(sc[1][:], res[1][1][:].indirect(cen_t[:]))
-        for b, blk in enumerate(halves):
-            nc.vector.tensor_tensor(prod[1][0][:, blk], res[1][2][:].indirect(pos_t[0][:, 8 * b:8 * b + 8]), gc[1][:, blk], MULT)
-        back = []
-        for b, blk in enumerate(halves):
-            turned = bank((7, 2)[b])
-            turn(turned[:, 0:P], sc[1][:, blk], True, False)
-            turn(turned[:, 0:P], prod[1][0][:, blk], False, True)
-            nc.scalar.activation(act1[0][:, blk], turned[:, 0:P], SILU)
-        for b, blk in enumerate(halves):
-            back.append(bank(3 + b))
-            turn(back[b][:, 0:P], act1[0][:, blk], True, True)
-        for b, blk in enumerate(halves):
-            nc.vector.tensor_tensor(prod[1][1][:, blk], res[1][2][:].indirect(pos_t[1][:, 8 * b:8 * b + 8]), gc[1][:, blk], MULT)
-        for blk, spare in zip(halves, (prod[1][0][:, halves[1]], prod[1][1][:, halves[0]])):
-            nc.vector.tensor_tensor(spare, prod[1][1][:, blk], sc[1][:, blk], ADD)
-            nc.scalar.activation(act1[1][:, blk], spare, SILU)
-        for b, blk in enumerate(halves):
-            nc.vector.tensor_tensor(out1[:, blk], act1[1][:, blk], back[b][:, 0:P], ADD)
-            nc.sync.dma_start(out[P:2 * P, blk], out1[:, blk])
+        nc.vector.tensor_copy(sc[1][:, left], res[1][1][:].indirect(places(cen_t, left)))
+        for d in range(2):
+            nc.vector.tensor_tensor(prod_left[d], res[1][2][:].indirect(places(pos_t[d], left)), gc[1][:, left], MULT)
+        for d in range(2):
+            nc.vector.tensor_tensor(prod[1][d][:, right], res[1][2][:].indirect(places(pos_t[d], right)), gc[1][:, right], MULT)
+        turned = [bank(t) for t in (7, 1)]
+        for d in range(2):
+            turn(turned[d][:, 0:P], sc[1][:, left], True, False)
+        back = bank(2)
+        for d in range(2):
+            turn(turned[d][:, 0:P], prod_left[d], False, True)
+            nc.scalar.activation(act1[d][:], turned[d][:, 0:P], SILU)
+        for d in range(2):
+            turn(back[:, 0:P], act1[d][:], d == 0, d == 1)
+        for d in range(2):
+            nc.vector.tensor_tensor(pre1[d][:], res[1][1][:].indirect(places(cen_t, right)), prod[1][d][:, right], ADD)
+        for d in range(2):
+            nc.scalar.activation(reused[:, halves[d]], pre1[d][:], SILU)
+        nc.vector.tensor_copy(out0[:], total[:, 0:V])
+        nc.sync.dma_start(out[0:P, :], out0[:])
+        nc.vector.tensor_copy(out1[0][:], back[:, 0:P])
+        nc.sync.dma_start(out[P:2 * P, left], out1[0][:])
+        nc.vector.tensor_tensor(out1[1][:], reused[:, left], reused[:, right], ADD)
+        nc.sync.dma_start(out[P:2 * P, right], out1[1][:])

@@ -141,13 +141,15 @@ def tile_picked_filmg_silu_e_kernel(tc, xT, w1_words, w1_scales, w2_words, w2_sc
 
         act0 = keep.tile([P, 2, V], F32, name="act0")
         out0 = keep.tile([P, V], F32, name="out0")
-        for d, tag in enumerate((5, 6)):
-            pre = bank(tag)
-            for blk in halves:
-                turn(pre[:, blk], prod[0][d][:, blk], True, False)
-                turn(pre[:, blk], sc[0][:, blk], False, True)
-            nc.scalar.activation(act0[:, d, :], pre[:, 0:V], SILU)
-        total = bank(0)
+        pre = [[bank(t) for t in pair] for pair in ((5, 6), (7, 0))]
+        for d in range(2):
+            for b, blk in enumerate(halves):
+                turn(pre[d][b][:, 0:P], prod[0][d][:, blk], True, False)
+        for b, blk in enumerate(halves):
+            for d in range(2):
+                turn(pre[d][b][:, 0:P], sc[0][:, blk], False, True)
+                nc.scalar.activation(act0[:, d, blk], pre[d][b][:, 0:P], SILU)
+        total = bank(1)
         for blk in halves:
             for d in range(2):
                 turn(total[:, blk], act0[:, d, blk], d == 0, d == 1)
@@ -165,10 +167,10 @@ def tile_picked_filmg_silu_e_kernel(tc, xT, w1_words, w1_scales, w2_words, w2_sc
             nc.vector.tensor_tensor(prod_left[d], res[1][2][:].indirect(places(pos_t[d], left)), gc[1][:, left], MULT)
         for d in range(2):
             nc.vector.tensor_tensor(prod[1][d][:, right], res[1][2][:].indirect(places(pos_t[d], right)), gc[1][:, right], MULT)
-        turned = [bank(t) for t in (7, 1)]
+        turned = [bank(t) for t in (2, 3)]
         for d in range(2):
             turn(turned[d][:, 0:P], sc[1][:, left], True, False)
-        back = bank(2)
+        back = bank(4)
         for d in range(2):
             turn(turned[d][:, 0:P], prod_left[d], False, True)
             nc.scalar.activation(act1[d][:], turned[d][:, 0:P], SILU)

@@ -61,33 +61,34 @@ def tile_picked_filmg_silu_e_kernel(tc, xT, w1_words, w1_scales, w2_words, w2_sc
         make_identity(nc, ident[:], nomemset=True)
 
         Q = S // 4
-        low = keep.tile([P, 2, S], BF16, name="low")
-        high = keep.tile([P, 2, 3 * Q], BF16, name="high")
-        front = keep.tile([P, H, 4], BF16, name="front", align_bytes=64)
-        third = keep.tile([P, Q, 4], BF16, name="third", align_bytes=64)
-        last = keep.tile([P, Q, 4], BF16, name="last", align_bytes=64)
-        quarter = [front[:, 0:Q, :], front[:, Q:H, :], third[:], last[:]]
+        rows = keep.tile([P, 4, S], BF16, name="rows")
+        low, high = rows[:, 0:2, :], rows[:, 2:4, :]
+        woven = keep.tile([P, S, 4], BF16, name="woven", align_bytes=64)
+        quarter = [woven[:, a * Q:(a + 1) * Q, :] for a in range(4)]
         codes = keep.tile([P, S], U32, name="codes", align_bytes=64)
         scales = keep.tile([P, S], U8, name="scales", align_bytes=64)
 
         def entries(first, count):
             return offs_t[:, first // 16:(first + count) // 16]
 
-        rounded = keep.tile([P, T], BF16, name="rounded")
-        nc.scalar.copy(rounded[:], raw[0][:])
-        nc.scalar.activation(low[:, 0, 3 * Q:S], rounded[:].indirect(entries(3 * Q, Q)), COPY)
-        nc.vector.tensor_copy(low[:, 0, 0:3 * Q], raw[0][:].indirect(entries(0, 3 * Q)))
-        for a in range(2):
-            nc.vector.tensor_copy(low[:, 1, a * H:(a + 1) * H], raw[1][:].indirect(entries(a * H, H)))
-        nc.scalar.copy(front[:, :, 0:2], low[:, :, 0:H].rearrange("p j w -> p w j"))
-        for a in range(2, 4):
-            nc.scalar.copy(quarter[a][:, :, 0:2], low[:, :, a * Q:(a + 1) * Q].rearrange("p j w -> p w j"))
-        nc.vector.tensor_copy(high[:, 0, :], raw[2][:].indirect(entries(0, 3 * Q)))
-        nc.vector.tensor_copy(last[:, :, 2], raw[2][:].indirect(entries(3 * Q, Q)))
-        for a in range(3):
+        rounded = [keep.tile([P, T], BF16, name="rounded%d" % j) for j in (0, 2)]
+        share = 192
+        nc.scalar.copy(rounded[0][:, 0:T // 2], raw[0][:, 0:T // 2])
+        nc.gpsimd.tensor_copy(rounded[0][:, T // 2:T], raw[0][:, T // 2:T])
+        nc.scalar.activation(low[:, 0, Q:H], rounded[0][:].indirect(entries(Q, Q)), COPY)
+        nc.vector.tensor_copy(low[:, 0, 0:Q], raw[0][:].indirect(entries(0, Q)))
+        nc.vector.tensor_copy(low[:, 0, H:S], raw[0][:].indirect(entries(H, H)))
+        for a, b in ((0, 192), (192, S)):
+            nc.vector.tensor_copy(low[:, 1, a:b], raw[1][:].indirect(entries(a, b - a)))
+            nc.scalar.copy(woven[:, a:b, 0:2], low[:, :, a:b].rearrange("p j w -> p w j"))
+        nc.gpsimd.tensor_copy(rounded[1][:], raw[2][:])
+        nc.scalar.activation(high[:, 0, 3 * Q - share:3 * Q], rounded[1][:].indirect(entries(3 * Q - share, share)), COPY)
+        nc.vector.tensor_copy(high[:, 0, 0:3 * Q - share], raw[2][:].indirect(entries(0, 3 * Q - share)))
+        nc.vector.tensor_copy(quarter[3][:, :, 2], raw[2][:].indirect(entries(3 * Q, Q)))
+        for a, weave in enumerate((nc.gpsimd.tensor_copy, nc.scalar.copy, nc.scalar.copy)):
             nc.vector.tensor_copy(high[:, 1, a * Q:(a + 1) * Q], raw[3][:].indirect(entries(a * Q, Q)))
-            nc.scalar.copy(quarter[a][:, :, 2:4], high[:, :, a * Q:(a + 1) * Q].rearrange("p j w -> p w j"))
-        nc.vector.tensor_copy(last[:, :, 3], raw[3][:].indirect(entries(3 * Q, Q)))
+            weave(quarter[a][:, :, 2:4], high[:, :, a * Q:(a + 1) * Q].rearrange("p j w -> p w j"))
+        nc.vector.tensor_copy(quarter[3][:, :, 3], raw[3][:].indirect(entries(3 * Q, Q)))
         first, second, whole = slice(0, H), slice(H, S), slice(0, S)
         cols_of = [slice(a * Q, (a + 1) * Q) for a in range(4)]
         order = (0, 1, 3, 2)
@@ -111,10 +112,11 @@ def tile_picked_filmg_silu_e_kernel(tc, xT, w1_words, w1_scales, w2_words, w2_sc
         for b, a in enumerate(order[:3]):
             nc.vector.tensor_copy(res[0][0][:, cols_of[a]], product(0, 0, cols_of[a], b))
         nc.scalar.copy(res[0][0][:, cols_of[order[3]]], product(0, 0, cols_of[order[3]], 3))
-        nc.scalar.copy(res[0][2][:, second], product(0, 2, second, 4))
-        nc.scalar.copy(res[0][2][:, first], product(0, 2, first, 0))
-        nc.scalar.copy(res[0][1][:], product(0, 1, whole, 1))
-        for i, b in enumerate((2, 3, 4)):
+        nc.scalar.copy(res[0][1][:, second], product(0, 1, second, 4))
+        nc.scalar.copy(res[0][1][:, first], product(0, 1, first, 0))
+        nc.scalar.copy(res[0][2][:, first], product(0, 2, first, 1))
+        nc.scalar.copy(res[0][2][:, second], product(0, 2, second, 2))
+        for i, b in enumerate((3, 4, 0)):
             nc.scalar.copy(res[1][i][:], product(1, i, whole, b))
 
         gc = [keep.tile([P, V], F32, name="gc%d" % m) for m in range(2)]
@@ -126,12 +128,10 @@ def tile_picked_filmg_silu_e_kernel(tc, xT, w1_words, w1_scales, w2_words, w2_sc
         def places(lst, blk):
             return lst[:, blk.start // 16:blk.stop // 16]
 
-        for blk in halves:
-            nc.vector.tensor_copy(gc[0][:, blk], res[0][0][:].indirect(places(cen_t, blk)))
-        for blk in halves:
-            nc.vector.tensor_tensor(prod[0][0][:, blk], res[0][2][:].indirect(places(pos_t[0], blk)), gc[0][:, blk], MULT)
-        nc.vector.tensor_tensor(prod[0][1][:], res[0][2][:].indirect(pos_t[1][:]), gc[0][:], MULT)
+        nc.vector.tensor_copy(gc[0][:], res[0][0][:].indirect(cen_t[:]))
         nc.vector.tensor_copy(sc[0][:], res[0][1][:].indirect(cen_t[:]))
+        for d in range(2):
+            nc.vector.tensor_tensor(prod[0][d][:], res[0][2][:].indirect(pos_t[d][:]), gc[0][:], MULT)
 
         def bank(tag):
             return psum.tile([P, S], F32, name="acc", tag="bank%d" % tag)
@@ -141,18 +141,20 @@ def tile_picked_filmg_silu_e_kernel(tc, xT, w1_words, w1_scales, w2_words, w2_sc
 
         act0 = keep.tile([P, 2, V], F32, name="act0")
         out0 = keep.tile([P, V], F32, name="out0")
-        pre = [[bank(t) for t in pair] for pair in ((5, 6), (7, 0))]
+        pre = [[bank(t) for t in pair] for pair in ((5, 6), (7, 1))]
         for d in range(2):
             for b, blk in enumerate(halves):
-                turn(pre[d][b][:, 0:P], prod[0][d][:, blk], True, False)
-        for b, blk in enumerate(halves):
-            for d in range(2):
-                turn(pre[d][b][:, 0:P], sc[0][:, blk], False, True)
+                turn(pre[d][b][:, 0:P], sc[0][:, blk], True, False)
+        for d in range(2):
+            for b, blk in enumerate(halves):
+                turn(pre[d][b][:, 0:P], prod[0][d][:, blk], False, True)
                 nc.scalar.activation(act0[:, d, blk], pre[d][b][:, 0:P], SILU)
-        total = bank(1)
+        total = bank(2)
         for blk in halves:
             for d in range(2):
                 turn(total[:, blk], act0[:, d, blk], d == 0, d == 1)
+        nc.scalar.copy(out0[:], total[:, 0:V])
+        nc.sync.dma_start(out[0:P, :], out0[:])
 
         left, right = halves
 
@@ -167,10 +169,10 @@ def tile_picked_filmg_silu_e_kernel(tc, xT, w1_words, w1_scales, w2_words, w2_sc
             nc.vector.tensor_tensor(prod_left[d], res[1][2][:].indirect(places(pos_t[d], left)), gc[1][:, left], MULT)
         for d in range(2):
             nc.vector.tensor_tensor(prod[1][d][:, right], res[1][2][:].indirect(places(pos_t[d], right)), gc[1][:, right], MULT)
-        turned = [bank(t) for t in (2, 3)]
+        turned = [bank(t) for t in (5, 6)]
         for d in range(2):
             turn(turned[d][:, 0:P], sc[1][:, left], True, False)
-        back = bank(4)
+        back = bank(3)
         for d in range(2):
             turn(turned[d][:, 0:P], prod_left[d], False, True)
             nc.scalar.activation(act1[d][:], turned[d][:, 0:P], SILU)
@@ -180,8 +182,6 @@ def tile_picked_filmg_silu_e_kernel(tc, xT, w1_words, w1_scales, w2_words, w2_sc
             nc.vector.tensor_tensor(pre1[d][:], res[1][1][:].indirect(places(cen_t, right)), prod[1][d][:, right], ADD)
         for d in range(2):
             nc.scalar.activation(reused[:, halves[d]], pre1[d][:], SILU)
-        nc.vector.tensor_copy(out0[:], total[:, 0:V])
-        nc.sync.dma_start(out[0:P, :], out0[:])
         nc.vector.tensor_copy(out1[0][:], back[:, 0:P])
         nc.sync.dma_start(out[P:2 * P, left], out1[0][:])
         nc.vector.tensor_tensor(out1[1][:], reused[:, left], reused[:, right], ADD)

@@ -21,6 +21,9 @@ SILU = mybir.ActivationFunctionType.Silu
 
 P = 128
 H = S // 2
+Q = S // 4
+SCALAR_WEAVE = 64
+G, SH, HN = 0, 1, 2
 
 
 def tile_picked_filmg_silu_e_kernel(tc, xT, w1_words, w1_scales, w2_words, w2_scales, w3_words, w3_scales, offs, cen, pos1, pos2, out):
@@ -35,18 +38,18 @@ def tile_picked_filmg_silu_e_kernel(tc, xT, w1_words, w1_scales, w2_words, w2_sc
         raw = [keep.tile([P, T], F32, name="raw%d" % j) for j in range(4)]
         planes = xT.rearrange("(p j) t -> j p t", j=4)
         w_scales = keep.tile([P, 3 * N], U8, name="w_scales", align_bytes=64)
+        w_words = [keep.tile([P, 2 * N], U8, name="w_words%d" % i, align_bytes=64) for i in range(3)]
         nc.vector.memset(w_scales[:].bitcast(I32), 0)
         nc.sync.dma_start(raw[0][:], planes[0])
         nc.sync.dma_start(offs_t[:], offs)
-        for j in (1, 2):
-            nc.sync.dma_start(raw[j][:], planes[j])
+        nc.sync.dma_start(raw[1][:], planes[1])
         for i, sc in enumerate((w1_scales, w2_scales, w3_scales)):
             nc.sync.dma_start(w_scales[0:16, i * N:(i + 1) * N].bitcast(I32), sc[0].bitcast(I32))
-        nc.sync.dma_start(raw[3][:], planes[3])
-        w_words = [keep.tile([P, 2 * N], U8, name="w_words%d" % i, align_bytes=64) for i in range(3)]
-        for i, w in enumerate((w1_words, w2_words, w3_words)):
-            nc.sync.dma_start(w_words[i][:].bitcast(I32), w[0].bitcast(I32))
-
+        for j in (2, 3):
+            nc.sync.dma_start(raw[j][:], planes[j])
+        words = (w1_words, w2_words, w3_words)
+        for i in (G, HN, SH):
+            nc.sync.dma_start(w_words[i][:].bitcast(I32), words[i][0].bitcast(I32))
         for q in range(1, 4):
             nc.sync.dma_start(w_scales[32 * q:32 * q + 4, :].bitcast(I32), w_scales[4 * q:4 * q + 4, :].bitcast(I32))
         nc.sync.dma_start(cen_t[:], cen)
@@ -60,129 +63,131 @@ def tile_picked_filmg_silu_e_kernel(tc, xT, w1_words, w1_scales, w2_words, w2_sc
         nc.vector.memset(ident[:], 0.0)
         make_identity(nc, ident[:], nomemset=True)
 
-        Q = S // 4
-        rows = keep.tile([P, 4, S], BF16, name="rows")
-        low, high = rows[:, 0:2, :], rows[:, 2:4, :]
+        def places(lst, first, count):
+            return lst[:, first // 16:(first + count) // 16]
+
         woven = keep.tile([P, S, 4], BF16, name="woven", align_bytes=64)
-        quarter = [woven[:, a * Q:(a + 1) * Q, :] for a in range(4)]
+        rows = keep.tile([P, 4, H], BF16, name="rows")
         codes = keep.tile([P, S], U32, name="codes", align_bytes=64)
         scales = keep.tile([P, S], U8, name="scales", align_bytes=64)
 
-        def entries(first, count):
-            return offs_t[:, first // 16:(first + count) // 16]
+        def weave(copy, first, count, pair):
+            cols = slice(first - H, first - H + count)
+            copy(woven[:, first:first + count, 2 * pair:2 * pair + 2], rows[:, 2 * pair:2 * pair + 2, cols].rearrange("p j w -> p w j"))
 
-        rounded = [keep.tile([P, T], BF16, name="rounded%d" % j) for j in (0, 2)]
-        share = 192
-        nc.scalar.copy(rounded[0][:, 0:T // 2], raw[0][:, 0:T // 2])
-        nc.gpsimd.tensor_copy(rounded[0][:, T // 2:T], raw[0][:, T // 2:T])
-        nc.scalar.activation(low[:, 0, Q:H], rounded[0][:].indirect(entries(Q, Q)), COPY)
-        nc.vector.tensor_copy(low[:, 0, 0:Q], raw[0][:].indirect(entries(0, Q)))
-        nc.vector.tensor_copy(low[:, 0, H:S], raw[0][:].indirect(entries(H, H)))
-        for a, b in ((0, 192), (192, S)):
-            nc.vector.tensor_copy(low[:, 1, a:b], raw[1][:].indirect(entries(a, b - a)))
-            nc.scalar.copy(woven[:, a:b, 0:2], low[:, :, a:b].rearrange("p j w -> p w j"))
-        nc.gpsimd.tensor_copy(rounded[1][:], raw[2][:])
-        nc.scalar.activation(high[:, 0, 3 * Q - share:3 * Q], rounded[1][:].indirect(entries(3 * Q - share, share)), COPY)
-        nc.vector.tensor_copy(high[:, 0, 0:3 * Q - share], raw[2][:].indirect(entries(0, 3 * Q - share)))
-        nc.vector.tensor_copy(quarter[3][:, :, 2], raw[2][:].indirect(entries(3 * Q, Q)))
-        for a, weave in enumerate((nc.gpsimd.tensor_copy, nc.scalar.copy, nc.scalar.copy)):
-            nc.vector.tensor_copy(high[:, 1, a * Q:(a + 1) * Q], raw[3][:].indirect(entries(a * Q, Q)))
-            weave(quarter[a][:, :, 2:4], high[:, :, a * Q:(a + 1) * Q].rearrange("p j w -> p w j"))
-        nc.vector.tensor_copy(quarter[3][:, :, 3], raw[3][:].indirect(entries(3 * Q, Q)))
-        first, second, whole = slice(0, H), slice(H, S), slice(0, S)
-        cols_of = [slice(a * Q, (a + 1) * Q) for a in range(4)]
-        order = (0, 1, 3, 2)
-        for a in order:
-            nc.vector.quantize_mx(out=codes[:, cols_of[a]].bitcast(FP8X4), scales=scales[:, cols_of[a]], in_=quarter[a].rearrange("p w j -> p (w j)"))
+        def stepped(j, first, count):
+            nc.vector.tensor_copy(woven[:, first:first + count, j], raw[j][:].indirect(places(offs_t, first, count)))
+
+        def plain(j, first, count):
+            nc.scalar.activation(rows[:, j, first - H:first - H + count], raw[j][:].indirect(places(offs_t, first, count)), COPY)
+
+        for j in range(3):
+            stepped(j, 0, H)
+            plain(j, H, H)
+            if j == 1:
+                weave(nc.gpsimd.tensor_copy, H, H - SCALAR_WEAVE, 0)
+                weave(nc.scalar.copy, S - SCALAR_WEAVE, SCALAR_WEAVE, 0)
+        for a in range(2):
+            stepped(3, a * Q, Q)
+            plain(3, H + a * Q, Q)
+        for a in (2, 3):
+            weave(nc.scalar.copy, a * Q, Q, 1)
+        quarters = [slice(a * Q, (a + 1) * Q) for a in range(4)]
+        for cols in quarters:
+            nc.vector.quantize_mx(out=codes[:, cols].bitcast(FP8X4), scales=scales[:, cols], in_=woven[:, cols, :].rearrange("p w j -> p (w j)"))
 
         res = [[keep.tile([P, S], F32, name="res%d_%d" % (m, i)) for i in range(3)] for m in range(2)]
 
-        def product(m, i, cols, bank):
-            width = cols.stop - cols.start
-            acc = psum.tile([P, S], F32, name="acc", tag="bank%d" % bank)
+        def bank(tag):
+            return psum.tile([P, S], F32, name="acc", tag="bank%d" % tag)
+
+        def product(m, i, cols, acc):
             nc.tensor.matmul_mx(
-                out=acc[:, 0:width],
+                out=acc,
                 lhsT=w_words[i][:, 2 * P * m:2 * P * (m + 1)].bitcast(FP4X4),
                 lhsT_scale=w_scales[:, i * N + P * m:i * N + P * (m + 1)],
                 rhs=codes[:, cols].bitcast(FP8X4),
                 rhs_scale=scales[:, cols],
                 start=True, stop=True)
-            return acc[:, 0:width]
 
-        for b, a in enumerate(order[:3]):
-            nc.vector.tensor_copy(res[0][0][:, cols_of[a]], product(0, 0, cols_of[a], b))
-        nc.scalar.copy(res[0][0][:, cols_of[order[3]]], product(0, 0, cols_of[order[3]], 3))
-        nc.scalar.copy(res[0][1][:, second], product(0, 1, second, 4))
-        nc.scalar.copy(res[0][1][:, first], product(0, 1, first, 0))
-        nc.scalar.copy(res[0][2][:, first], product(0, 2, first, 1))
-        nc.scalar.copy(res[0][2][:, second], product(0, 2, second, 2))
-        for i, b in enumerate((3, 4, 0)):
-            nc.scalar.copy(res[1][i][:], product(1, i, whole, b))
+        def piece(m, i, cols, tag, copy):
+            acc = bank(tag)[:, 0:cols.stop - cols.start]
+            product(m, i, cols, acc)
+            copy(res[m][i][:, cols], acc)
+
+        def rest(m, i, tag):
+            acc = bank(tag)
+            for cols in (slice(H, S), quarters[1]):
+                product(m, i, cols, acc[:, cols])
+            nc.scalar.copy(res[m][i][:, Q:S], acc[:, Q:S])
+
+        early = [bank(0), bank(1)]
+        firsts = ((0, G), (0, HN), (0, SH), (1, G))
+        for a, (m, i) in enumerate(firsts):
+            product(m, i, quarters[0], early[a // 2][:, quarters[a % 2]])
+        for a, (m, i) in enumerate(firsts):
+            copy = nc.scalar.copy if a < 2 else nc.vector.tensor_copy
+            copy(res[m][i][:, quarters[0]], early[a // 2][:, quarters[a % 2]])
+        piece(0, G, quarters[1], 2, nc.vector.tensor_copy)
+        for a in (2, 3):
+            piece(0, G, quarters[a], a + 1, nc.scalar.copy)
+        rest(0, HN, 5)
 
         gc = [keep.tile([P, V], F32, name="gc%d" % m) for m in range(2)]
-        sc = [keep.tile([P, V], F32, name="sc%d" % m) for m in range(2)]
-        prod = [[keep.tile([P, V], F32, name="prod%d_%d" % (m, d)) for d in range(2)] for m in range(2)]
-
-        halves = [slice(b * P, (b + 1) * P) for b in range(2)]
-
-        def places(lst, blk):
-            return lst[:, blk.start // 16:blk.stop // 16]
-
-        nc.vector.tensor_copy(gc[0][:], res[0][0][:].indirect(cen_t[:]))
-        nc.vector.tensor_copy(sc[0][:], res[0][1][:].indirect(cen_t[:]))
-        for d in range(2):
-            nc.vector.tensor_tensor(prod[0][d][:], res[0][2][:].indirect(pos_t[d][:]), gc[0][:], MULT)
-
-        def bank(tag):
-            return psum.tile([P, S], F32, name="acc", tag="bank%d" % tag)
+        sc0 = [keep.tile([P, V], F32, name="sc0_left", tag="sc"), keep.tile([P, P], F32, name="sc0_right")]
+        prod = [[keep.tile([P, V], F32, name="prod%d" % d) for d in range(2)]]
+        left, right = halves = [slice(b * P, (b + 1) * P) for b in range(2)]
 
         def turn(acc, block, start, stop):
             nc.tensor.matmul(acc, block, ident[:], start=start, stop=stop, is_transpose=True)
 
+        for blk in halves:
+            nc.vector.tensor_copy(gc[0][:, blk], res[0][G][:].indirect(places(cen_t, blk.start, P)))
+        nc.vector.tensor_tensor(prod[0][0][:, left], res[0][HN][:].indirect(places(pos_t[0], 0, P)), gc[0][:, left], MULT)
+        nc.vector.tensor_tensor(prod[0][0][:, right], res[0][HN][:].indirect(places(pos_t[0], P, P)), gc[0][:, right], MULT)
+        nc.vector.tensor_tensor(prod[0][1][:], res[0][HN][:].indirect(pos_t[1][:]), gc[0][:], MULT)
+        rest(0, SH, 6)
+        rest(1, G, 7)
+        for b, blk in enumerate(halves):
+            nc.scalar.activation(sc0[b][:, 0:P], res[0][SH][:].indirect(places(cen_t, blk.start, P)), COPY)
+        nc.scalar.activation(gc[1][:], res[1][G][:].indirect(cen_t[:]), COPY)
+        piece(1, HN, slice(0, S), 6, nc.vector.tensor_copy)
+        piece(1, SH, slice(0, H), 7, nc.vector.tensor_copy)
+        piece(1, SH, slice(H, S), 4, nc.scalar.copy)
+
         act0 = keep.tile([P, 2, V], F32, name="act0")
         out0 = keep.tile([P, V], F32, name="out0")
-        pre = [[bank(t) for t in pair] for pair in ((5, 6), (7, 1))]
+        pre = [bank(b) for b in (2, 3)]
         for d in range(2):
             for b, blk in enumerate(halves):
-                turn(pre[d][b][:, 0:P], sc[0][:, blk], True, False)
-        for d in range(2):
-            for b, blk in enumerate(halves):
-                turn(pre[d][b][:, 0:P], prod[0][d][:, blk], False, True)
-                nc.scalar.activation(act0[:, d, blk], pre[d][b][:, 0:P], SILU)
-        total = bank(2)
-        for blk in halves:
+                turn(pre[b][:, halves[d]], prod[0][d][:, blk], d == 0, False)
+        for b in range(2):
             for d in range(2):
-                turn(total[:, blk], act0[:, d, blk], d == 0, d == 1)
-        nc.scalar.copy(out0[:], total[:, 0:V])
-        nc.sync.dma_start(out[0:P, :], out0[:])
+                turn(pre[b][:, halves[d]], sc0[b][:, 0:P], False, d == 1)
+        total = [bank(b) for b in (5, 0)]
 
-        left, right = halves
+        def finish(b):
+            nc.scalar.activation(act0[:, b, :], pre[b][:, 0:V], SILU)
+            for d in range(2):
+                turn(total[b][:, 0:P], act0[:, b, halves[d]], d == 0, d == 1)
 
+        finish(0)
+        sc1 = keep.tile([P, V], F32, name="sc1", tag="sc")
+        nc.scalar.activation(sc1[:], res[1][SH][:].indirect(cen_t[:]), COPY)
+        finish(1)
+
+        both = keep.tile([P, 2, V], F32, name="both")
+        pre1 = keep.tile([P, 2, V], F32, name="pre1")
+        act1 = keep.tile([P, 2, V], F32, name="act1")
         out1 = [keep.tile([P, P], F32, name="out1_%d" % b) for b in range(2)]
-        act1 = [keep.tile([P, P], F32, name="act1_%d" % d) for d in range(2)]
-        pre1 = [keep.tile([P, P], F32, name="pre1_%d" % d) for d in range(2)]
-        reused = keep.tile([P, V], F32, name="reused")
-        prod_left = [prod[1][0][:, left], reused[:, P // 2:P // 2 + P]]
-        nc.vector.tensor_copy(gc[1][:], res[1][0][:].indirect(cen_t[:]))
-        nc.vector.tensor_copy(sc[1][:, left], res[1][1][:].indirect(places(cen_t, left)))
         for d in range(2):
-            nc.vector.tensor_tensor(prod_left[d], res[1][2][:].indirect(places(pos_t[d], left)), gc[1][:, left], MULT)
-        for d in range(2):
-            nc.vector.tensor_tensor(prod[1][d][:, right], res[1][2][:].indirect(places(pos_t[d], right)), gc[1][:, right], MULT)
-        turned = [bank(t) for t in (5, 6)]
-        for d in range(2):
-            turn(turned[d][:, 0:P], sc[1][:, left], True, False)
-        back = bank(3)
-        for d in range(2):
-            turn(turned[d][:, 0:P], prod_left[d], False, True)
-            nc.scalar.activation(act1[d][:], turned[d][:, 0:P], SILU)
-        for d in range(2):
-            turn(back[:, 0:P], act1[d][:], d == 0, d == 1)
-        for d in range(2):
-            nc.vector.tensor_tensor(pre1[d][:], res[1][1][:].indirect(places(cen_t, right)), prod[1][d][:, right], ADD)
-        for d in range(2):
-            nc.scalar.activation(reused[:, halves[d]], pre1[d][:], SILU)
-        nc.vector.tensor_copy(out1[0][:], back[:, 0:P])
-        nc.sync.dma_start(out[P:2 * P, left], out1[0][:])
-        nc.vector.tensor_tensor(out1[1][:], reused[:, left], reused[:, right], ADD)
-        nc.sync.dma_start(out[P:2 * P, right], out1[1][:])
+            nc.vector.tensor_tensor(both[:, d, :], res[1][HN][:].indirect(pos_t[d][:]), gc[1][:], MULT)
+        for d, blk in ((0, slice(0, V)), (1, left), (1, right)):
+            nc.vector.tensor_tensor(pre1[:, d, blk], both[:, d, blk], sc1[:, blk], ADD)
+            nc.scalar.activation(act1[:, d, blk], pre1[:, d, blk], SILU)
+        for b, blk in enumerate(halves):
+            nc.vector.tensor_copy(out0[:, blk], total[b][:, 0:P])
+        nc.sync.dma_start(out[0:P, :], out0[:])
+        for b, blk in enumerate(halves):
+            nc.vector.tensor_tensor(out1[b][:], act1[:, 0, blk], act1[:, 1, blk], ADD)
+            nc.sync.dma_start(out[P:2 * P, blk], out1[b][:])

@@ -158,12 +158,11 @@ def tile_picked_filmg_silu_e_kernel(tc, xT, w1_words, w1_scales, w2_words, w2_sc
         act0 = keep.tile([P, 2, V], F32, name="act0")
         out0 = keep.tile([P, V], F32, name="out0")
         pre = [bank(b) for b in (2, 3)]
-        for d in range(2):
-            for b, blk in enumerate(halves):
-                turn(pre[b][:, halves[d]], prod[0][d][:, blk], d == 0, False)
-        for b in range(2):
+        for b, blk in enumerate(halves):
             for d in range(2):
-                turn(pre[b][:, halves[d]], sc0[b][:, 0:P], False, d == 1)
+                turn(pre[b][:, halves[d]], sc0[b][:, 0:P], d == 0, False)
+            for d in range(2):
+                turn(pre[b][:, halves[d]], prod[0][d][:, blk], False, d == 1)
         total = [bank(b) for b in (5, 0)]
 
         def finish(b):

@@ -90,11 +90,13 @@ def tile_picked_filmg_silu_e_kernel(tc, xT, w1_words, w1_scales, w2_words, w2_sc
         for a in range(2):
             stepped(3, a * Q, Q)
             plain(3, H + a * Q, Q)
-        for a in (2, 3):
-            weave(nc.scalar.copy, a * Q, Q, 1)
+        weave(nc.scalar.copy, H, Q, 1)
+        weave(nc.scalar.copy, H + Q, Q - SCALAR_WEAVE, 1)
         quarters = [slice(a * Q, (a + 1) * Q) for a in range(4)]
-        for cols in quarters:
+        for a, cols in enumerate(quarters):
             nc.vector.quantize_mx(out=codes[:, cols].bitcast(FP8X4), scales=scales[:, cols], in_=woven[:, cols, :].rearrange("p w j -> p (w j)"))
+            if a == 0:
+                weave(nc.vector.tensor_copy, S - SCALAR_WEAVE, SCALAR_WEAVE, 1)
 
         res = [[keep.tile([P, S], F32, name="res%d_%d" % (m, i)) for i in range(3)] for m in range(2)]
 
@@ -134,7 +136,7 @@ def tile_picked_filmg_silu_e_kernel(tc, xT, w1_words, w1_scales, w2_words, w2_sc
         rest(0, HN, 5)
 
         gc = [keep.tile([P, V], F32, name="gc%d" % m) for m in range(2)]
-        sc0 = [keep.tile([P, V], F32, name="sc0_left", tag="sc"), keep.tile([P, P], F32, name="sc0_right")]
+        sc0 = keep.tile([P, V], F32, name="sc0", tag="sc")
         prod = [[keep.tile([P, V], F32, name="prod%d" % d) for d in range(2)]]
         left, right = halves = [slice(b * P, (b + 1) * P) for b in range(2)]
 
@@ -148,22 +150,22 @@ def tile_picked_filmg_silu_e_kernel(tc, xT, w1_words, w1_scales, w2_words, w2_sc
         nc.vector.tensor_tensor(prod[0][1][:], res[0][HN][:].indirect(pos_t[1][:]), gc[0][:], MULT)
         rest(0, SH, 6)
         rest(1, G, 7)
-        for b, blk in enumerate(halves):
-            nc.scalar.activation(sc0[b][:, 0:P], res[0][SH][:].indirect(places(cen_t, blk.start, P)), COPY)
+        nc.scalar.activation(sc0[:], res[0][SH][:].indirect(cen_t[:]), COPY)
         nc.scalar.activation(gc[1][:], res[1][G][:].indirect(cen_t[:]), COPY)
-        piece(1, HN, slice(0, S), 6, nc.vector.tensor_copy)
-        piece(1, SH, slice(0, H), 7, nc.vector.tensor_copy)
+        piece(1, HN, slice(0, S), 5, nc.vector.tensor_copy)
+        piece(1, SH, slice(0, H), 6, nc.vector.tensor_copy)
         piece(1, SH, slice(H, S), 4, nc.scalar.copy)
 
         act0 = keep.tile([P, 2, V], F32, name="act0")
         out0 = keep.tile([P, V], F32, name="out0")
         pre = [bank(b) for b in (2, 3)]
         for b, blk in enumerate(halves):
+            turn(pre[b][:, left], prod[0][0][:, blk], True, False)
+        for b, blk in enumerate(halves):
             for d in range(2):
-                turn(pre[b][:, halves[d]], sc0[b][:, 0:P], d == 0, False)
-            for d in range(2):
-                turn(pre[b][:, halves[d]], prod[0][d][:, blk], False, d == 1)
-        total = [bank(b) for b in (5, 0)]
+                turn(pre[b][:, halves[d]], sc0[:, blk], False, False)
+            turn(pre[b][:, right], prod[0][1][:, blk], False, True)
+        total = [bank(b) for b in (7, 0)]
 
         def finish(b):
             nc.scalar.activation(act0[:, b, :], pre[b][:, 0:V], SILU)

@@ -35,7 +35,7 @@ def tile_picked_filmg_silu_e_kernel(tc, xT, w1_words, w1_scales, w2_words, w2_sc
         offs_t = keep.tile([P, S // 16], U16, name="offs_t")
         cen_t = keep.tile([P, V // 16], U16, name="cen_t")
         pos_t = [keep.tile([P, V // 16], U16, name="pos_t%d" % d) for d in range(2)]
-        raw = [keep.tile([P, T], F32, name="raw%d" % j) for j in range(4)]
+        raw = [keep.tile([P, T], F32, name="raw%d" % j, align_bytes=256) for j in range(4)]
         planes = xT.rearrange("(p j) t -> j p t", j=4)
         w_scales = keep.tile([P, 3 * N], U8, name="w_scales", align_bytes=64)
         w_words = [keep.tile([P, 2 * N], U8, name="w_words%d" % i, align_bytes=64) for i in range(3)]

@@ -22,7 +22,6 @@ SILU = mybir.ActivationFunctionType.Silu
 P = 128
 H = S // 2
 Q = S // 4
-SCALAR_WEAVE = 64
 G, SH, HN = 0, 1, 2
 
 
@@ -67,36 +66,24 @@ def tile_picked_filmg_silu_e_kernel(tc, xT, w1_words, w1_scales, w2_words, w2_sc
             return lst[:, first // 16:(first + count) // 16]
 
         woven = keep.tile([P, S, 4], BF16, name="woven", align_bytes=64)
-        rows = keep.tile([P, 4, H], BF16, name="rows")
         codes = keep.tile([P, S], U32, name="codes", align_bytes=64)
         scales = keep.tile([P, S], U8, name="scales", align_bytes=64)
-
-        def weave(copy, first, count, pair):
-            cols = slice(first - H, first - H + count)
-            copy(woven[:, first:first + count, 2 * pair:2 * pair + 2], rows[:, 2 * pair:2 * pair + 2, cols].rearrange("p j w -> p w j"))
 
         def stepped(j, first, count):
             nc.vector.tensor_copy(woven[:, first:first + count, j], raw[j][:].indirect(places(offs_t, first, count)))
 
-        def plain(j, first, count):
-            nc.scalar.activation(rows[:, j, first - H:first - H + count], raw[j][:].indirect(places(offs_t, first, count)), COPY)
+        def stepped_scalar(j, first, count):
+            nc.scalar.activation(woven[:, first:first + count, j], raw[j][:].indirect(places(offs_t, first, count)), COPY)
 
         for j in range(3):
             stepped(j, 0, H)
-            plain(j, H, H)
-            if j == 1:
-                weave(nc.gpsimd.tensor_copy, H, H - SCALAR_WEAVE, 0)
-                weave(nc.scalar.copy, S - SCALAR_WEAVE, SCALAR_WEAVE, 0)
+            stepped_scalar(j, H, H)
         for a in range(2):
             stepped(3, a * Q, Q)
-            plain(3, H + a * Q, Q)
-        weave(nc.scalar.copy, H, Q, 1)
-        weave(nc.scalar.copy, H + Q, Q - SCALAR_WEAVE, 1)
+            stepped_scalar(3, H + a * Q, Q)
         quarters = [slice(a * Q, (a + 1) * Q) for a in range(4)]
-        for a, cols in enumerate(quarters):
+        for cols in quarters:
             nc.vector.quantize_mx(out=codes[:, cols].bitcast(FP8X4), scales=scales[:, cols], in_=woven[:, cols, :].rearrange("p w j -> p (w j)"))
-            if a == 0:
-                weave(nc.vector.tensor_copy, S - SCALAR_WEAVE, SCALAR_WEAVE, 1)
 
         res = [[keep.tile([P, S], F32, name="res%d_%d" % (m, i)) for i in range(3)] for m in range(2)]
 

@@ -22,6 +22,7 @@ SILU = mybir.ActivationFunctionType.Silu
 P = 128
 H = S // 2
 Q = S // 4
+MID = 192
 G, SH, HN = 0, 1, 2
 
 
@@ -39,12 +40,12 @@ def tile_picked_filmg_silu_e_kernel(tc, xT, w1_words, w1_scales, w2_words, w2_sc
         w_scales = keep.tile([P, 3 * N], U8, name="w_scales", align_bytes=64)
         w_words = [keep.tile([P, 2 * N], U8, name="w_words%d" % i, align_bytes=64) for i in range(3)]
         nc.vector.memset(w_scales[:].bitcast(I32), 0)
-        nc.sync.dma_start(raw[0][:], planes[0])
+        nc.sync.dma_start(raw[2][:], planes[2])
         nc.sync.dma_start(offs_t[:], offs)
-        nc.sync.dma_start(raw[1][:], planes[1])
+        nc.sync.dma_start(raw[0][:], planes[0])
         for i, sc in enumerate((w1_scales, w2_scales, w3_scales)):
             nc.sync.dma_start(w_scales[0:16, i * N:(i + 1) * N].bitcast(I32), sc[0].bitcast(I32))
-        for j in (2, 3):
+        for j in (1, 3):
             nc.sync.dma_start(raw[j][:], planes[j])
         words = (w1_words, w2_words, w3_words)
         for i in (G, HN, SH):
@@ -75,14 +76,19 @@ def tile_picked_filmg_silu_e_kernel(tc, xT, w1_words, w1_scales, w2_words, w2_sc
         def stepped_scalar(j, first, count):
             nc.scalar.activation(woven[:, first:first + count, j], raw[j][:].indirect(places(offs_t, first, count)), COPY)
 
-        for j in range(3):
+        stepped_scalar(2, 0, MID)
+        stepped(2, MID, MID)
+        stepped_scalar(2, 3 * Q, Q)
+        for j in (0, 1):
             stepped(j, 0, H)
             stepped_scalar(j, H, H)
-        for a in range(2):
-            stepped(3, a * Q, Q)
-            stepped_scalar(3, H + a * Q, Q)
+        stepped_scalar(3, 0, Q)
+        stepped(3, MID, MID)
+        stepped_scalar(3, Q, MID - Q)
+        stepped_scalar(3, 3 * Q, Q)
         quarters = [slice(a * Q, (a + 1) * Q) for a in range(4)]
-        for cols in quarters:
+        middle = slice(Q, 3 * Q)
+        for cols in (quarters[0], middle, quarters[3]):
             nc.vector.quantize_mx(out=codes[:, cols].bitcast(FP8X4), scales=scales[:, cols], in_=woven[:, cols, :].rearrange("p w j -> p (w j)"))
 
         res = [[keep.tile([P, S], F32, name="res%d_%d" % (m, i)) for i in range(3)] for m in range(2)]
@@ -106,20 +112,19 @@ def tile_picked_filmg_silu_e_kernel(tc, xT, w1_words, w1_scales, w2_words, w2_sc
 
         def rest(m, i, tag):
             acc = bank(tag)
-            for cols in (slice(H, S), quarters[1]):
+            for cols in (middle, quarters[3]):
                 product(m, i, cols, acc[:, cols])
             nc.scalar.copy(res[m][i][:, Q:S], acc[:, Q:S])
 
         early = [bank(0), bank(1)]
-        firsts = ((0, G), (0, HN), (0, SH), (1, G))
+        firsts = ((0, G), (0, HN), (0, SH))
         for a, (m, i) in enumerate(firsts):
             product(m, i, quarters[0], early[a // 2][:, quarters[a % 2]])
         for a, (m, i) in enumerate(firsts):
             copy = nc.scalar.copy if a < 2 else nc.vector.tensor_copy
             copy(res[m][i][:, quarters[0]], early[a // 2][:, quarters[a % 2]])
-        piece(0, G, quarters[1], 2, nc.vector.tensor_copy)
-        for a in (2, 3):
-            piece(0, G, quarters[a], a + 1, nc.scalar.copy)
+        piece(0, G, middle, 2, nc.vector.tensor_copy)
+        piece(0, G, quarters[3], 4, nc.scalar.copy)
         rest(0, HN, 5)
 
         gc = [keep.tile([P, V], F32, name="gc%d" % m) for m in range(2)]
@@ -136,7 +141,7 @@ def tile_picked_filmg_silu_e_kernel(tc, xT, w1_words, w1_scales, w2_words, w2_sc
         nc.vector.tensor_tensor(prod[0][0][:, right], res[0][HN][:].indirect(places(pos_t[0], P, P)), gc[0][:, right], MULT)
         nc.vector.tensor_tensor(prod[0][1][:], res[0][HN][:].indirect(pos_t[1][:]), gc[0][:], MULT)
         rest(0, SH, 6)
-        rest(1, G, 7)
+        piece(1, G, slice(0, S), 7, nc.scalar.copy)
         nc.scalar.activation(sc0[:], res[0][SH][:].indirect(cen_t[:]), COPY)
         nc.scalar.activation(gc[1][:], res[1][G][:].indirect(cen_t[:]), COPY)
         piece(1, HN, slice(0, S), 5, nc.vector.tensor_copy)

@@ -37,8 +37,8 @@ def tile_picked_filmg_silu_e_kernel(tc, xT, w1_words, w1_scales, w2_words, w2_sc
         pos_t = [keep.tile([P, V // 16], U16, name="pos_t%d" % d) for d in range(2)]
         raw = [keep.tile([P, T], F32, name="raw%d" % j, align_bytes=256) for j in range(4)]
         planes = xT.rearrange("(p j) t -> j p t", j=4)
-        w_scales = keep.tile([P, 3 * N], U8, name="w_scales", align_bytes=64)
-        w_words = [keep.tile([P, 2 * N], U8, name="w_words%d" % i, align_bytes=64) for i in range(3)]
+        w_scales = keep.tile([P, 3 * N], U8, name="w_scales", align_bytes=256)
+        w_words = [keep.tile([P, 2 * N], U8, name="w_words%d" % i, align_bytes=256) for i in range(3)]
         nc.vector.memset(w_scales[:].bitcast(I32), 0)
         nc.sync.dma_start(raw[2][:], planes[2])
         nc.sync.dma_start(offs_t[:], offs)
@@ -66,9 +66,9 @@ def tile_picked_filmg_silu_e_kernel(tc, xT, w1_words, w1_scales, w2_words, w2_sc
         def places(lst, first, count):
             return lst[:, first // 16:(first + count) // 16]
 
-        woven = keep.tile([P, S, 4], BF16, name="woven", align_bytes=64)
-        codes = keep.tile([P, S], U32, name="codes", align_bytes=64)
-        scales = keep.tile([P, S], U8, name="scales", align_bytes=64)
+        woven = keep.tile([P, S, 4], BF16, name="woven", align_bytes=256)
+        codes = keep.tile([P, S], U32, name="codes", align_bytes=256)
+        scales = keep.tile([P, S], U8, name="scales", align_bytes=256)
 
         def stepped(j, first, count):
             nc.vector.tensor_copy(woven[:, first:first + count, j], raw[j][:].indirect(places(offs_t, first, count)))
@@ -91,7 +91,7 @@ def tile_picked_filmg_silu_e_kernel(tc, xT, w1_words, w1_scales, w2_words, w2_sc
         for cols in (quarters[0], middle, quarters[3]):
             nc.vector.quantize_mx(out=codes[:, cols].bitcast(FP8X4), scales=scales[:, cols], in_=woven[:, cols, :].rearrange("p w j -> p (w j)"))
 
-        res = [[keep.tile([P, S], F32, name="res%d_%d" % (m, i)) for i in range(3)] for m in range(2)]
+        res = [[keep.tile([P, S], F32, name="res%d_%d" % (m, i), align_bytes=256) for i in range(3)] for m in range(2)]
 
         def bank(tag):
             return psum.tile([P, S], F32, name="acc", tag="bank%d" % tag)
@@ -149,14 +149,14 @@ def tile_picked_filmg_silu_e_kernel(tc, xT, w1_words, w1_scales, w2_words, w2_sc
         piece(1, SH, slice(H, S), 4, nc.scalar.copy)
 
         act0 = keep.tile([P, 2, V], F32, name="act0")
-        out0 = keep.tile([P, V], F32, name="out0")
+        out0 = keep.tile([P, V], F32, name="out0", align_bytes=256)
         pre = [bank(b) for b in (2, 3)]
-        for b, blk in enumerate(halves):
-            turn(pre[b][:, left], prod[0][0][:, blk], True, False)
+        for d in range(2):
+            for b, blk in enumerate(halves):
+                turn(pre[b][:, halves[d]], prod[0][d][:, blk], d == 0, False)
         for b, blk in enumerate(halves):
             for d in range(2):
-                turn(pre[b][:, halves[d]], sc0[:, blk], False, False)
-            turn(pre[b][:, right], prod[0][1][:, blk], False, True)
+                turn(pre[b][:, halves[d]], sc0[:, blk], False, d == 1)
         total = [bank(b) for b in (7, 0)]
 
         def finish(b):
@@ -172,7 +172,7 @@ def tile_picked_filmg_silu_e_kernel(tc, xT, w1_words, w1_scales, w2_words, w2_sc
         both = keep.tile([P, 2, V], F32, name="both")
         pre1 = keep.tile([P, 2, V], F32, name="pre1")
         act1 = keep.tile([P, 2, V], F32, name="act1")
-        out1 = [keep.tile([P, P], F32, name="out1_%d" % b) for b in range(2)]
+        out1 = [keep.tile([P, P], F32, name="out1_%d" % b, align_bytes=256) for b in range(2)]
         for d in range(2):
             nc.vector.tensor_tensor(both[:, d, :], res[1][HN][:].indirect(pos_t[d][:]), gc[1][:], MULT)
         for d, blk in ((0, slice(0, V)), (1, left), (1, right)):

@@ -80,8 +80,9 @@ def tile_picked_filmg_silu_e_kernel(tc, xT, w1_words, w1_scales, w2_words, w2_sc
         stepped(2, MID, MID)
         stepped_scalar(2, 3 * Q, Q)
         for j in (0, 1):
-            stepped(j, 0, H)
-            stepped_scalar(j, H, H)
+            stepped_scalar(j, 0, Q)
+            stepped(j, Q, H)
+            stepped_scalar(j, 3 * Q, Q)
         stepped_scalar(3, 0, Q)
         stepped(3, MID, MID)
         stepped_scalar(3, Q, MID - Q)

from contextlib import ExitStack

import concourse.mybir as mybir
from concourse.masks import make_identity

K, T, S, V, N = 512, 1024, 512, 256, 256
FLOPS = 3 * 2 * K * N * S

F32 = mybir.dt.float32
BF16 = mybir.dt.bfloat16
I32 = mybir.dt.int32
U32 = mybir.dt.uint32
U16 = mybir.dt.uint16
U8 = mybir.dt.uint8
FP8X4 = mybir.dt.float8_e4m3fn_x4
FP4X4 = mybir.dt.float4_e2m1fn_x4
MULT = mybir.AluOpType.mult
ADD = mybir.AluOpType.add
COPY = mybir.ActivationFunctionType.Copy
SILU = mybir.ActivationFunctionType.Silu

P = 128
H = S // 2
Q = S // 4
MID = 192
G, SH, HN = 0, 1, 2


def tile_picked_filmg_silu_e_kernel(tc, xT, w1_words, w1_scales, w2_words, w2_scales, w3_words, w3_scales, offs, cen, pos1, pos2, out):
    nc = tc.nc
    with ExitStack() as ctx:
        keep = ctx.enter_context(tc.tile_pool(name="keep", bufs=1))
        psum = ctx.enter_context(tc.psum_pool(name="psum", bufs=1))

        offs_t = keep.tile([P, S // 16], U16, name="offs_t")
        cen_t = keep.tile([P, V // 16], U16, name="cen_t")
        pos_t = [keep.tile([P, V // 16], U16, name="pos_t%d" % d) for d in range(2)]
        raw = [keep.tile([P, T], F32, name="raw%d" % j, align_bytes=256) for j in range(4)]
        planes = xT.rearrange("(p j) t -> j p t", j=4)
        w_scales = keep.tile([P, 3 * N], U8, name="w_scales", align_bytes=256)
        w_words = [keep.tile([P, 2 * N], U8, name="w_words%d" % i, align_bytes=256) for i in range(3)]
        nc.vector.memset(w_scales[:].bitcast(I32), 0)
        nc.sync.dma_start(raw[2][:], planes[2])
        nc.sync.dma_start(offs_t[:], offs)
        nc.sync.dma_start(raw[0][:], planes[0])
        for i, sc in enumerate((w1_scales, w2_scales, w3_scales)):
            nc.sync.dma_start(w_scales[0:16, i * N:(i + 1) * N].bitcast(I32), sc[0].bitcast(I32))
        for j in (1, 3):
            nc.sync.dma_start(raw[j][:], planes[j])
        words = (w1_words, w2_words, w3_words)
        for i in (G, HN, SH):
            nc.sync.dma_start(w_words[i][:].bitcast(I32), words[i][0].bitcast(I32))
        for q in range(1, 4):
            nc.sync.dma_start(w_scales[32 * q:32 * q + 4, :].bitcast(I32), w_scales[4 * q:4 * q + 4, :].bitcast(I32))
        nc.sync.dma_start(cen_t[:], cen)
        nc.sync.dma_start(pos_t[0][:], pos1)
        nc.sync.dma_start(pos_t[1][:], pos2)
        warm = keep.tile([P, 8], F32, name="warm")
        nc.vector.memset(warm[:, 0:1], 0.0)
        nc.scalar.activation(warm[:, 4:5], warm[:, 0:1], SILU)

        ident = keep.tile([P, P], F32, name="ident")
        nc.vector.memset(ident[:], 0.0)
        make_identity(nc, ident[:], nomemset=True)

        def places(lst, first, count):
            return lst[:, first // 16:(first + count) // 16]

        woven = keep.tile([P, S, 4], BF16, name="woven", align_bytes=256)
        codes = keep.tile([P, S], U32, name="codes", align_bytes=256)
        scales = keep.tile([P, S], U8, name="scales", align_bytes=256)

        def stepped(j, first, count):
            nc.vector.tensor_copy(woven[:, first:first + count, j], raw[j][:].indirect(places(offs_t, first, count)))

        def stepped_scalar(j, first, count):
            nc.scalar.activation(woven[:, first:first + count, j], raw[j][:].indirect(places(offs_t, first, count)), COPY)

        stepped_scalar(2, 0, MID)
        stepped(2, MID, MID)
        stepped_scalar(2, 3 * Q, Q)
        for j in (0, 1):
            stepped_scalar(j, 0, Q)
            stepped(j, Q, H)
            stepped_scalar(j, 3 * Q, Q)
        stepped_scalar(3, 0, Q)
        stepped(3, MID, MID)
        stepped_scalar(3, Q, MID - Q)
        stepped_scalar(3, 3 * Q, Q)
        quarters = [slice(a * Q, (a + 1) * Q) for a in range(4)]
        middle = slice(Q, 3 * Q)
        for cols in (quarters[0], middle, quarters[3]):
            nc.vector.quantize_mx(out=codes[:, cols].bitcast(FP8X4), scales=scales[:, cols], in_=woven[:, cols, :].rearrange("p w j -> p (w j)"))

        res = [[keep.tile([P, S], F32, name="res%d_%d" % (m, i), align_bytes=256) for i in range(3)] for m in range(2)]

        def bank(tag):
            return psum.tile([P, S], F32, name="acc", tag="bank%d" % tag)

        def product(m, i, cols, acc):
            nc.tensor.matmul_mx(
                out=acc,
                lhsT=w_words[i][:, 2 * P * m:2 * P * (m + 1)].bitcast(FP4X4),
                lhsT_scale=w_scales[:, i * N + P * m:i * N + P * (m + 1)],
                rhs=codes[:, cols].bitcast(FP8X4),
                rhs_scale=scales[:, cols],
                start=True, stop=True)

        def piece(m, i, cols, tag, copy):
            acc = bank(tag)[:, 0:cols.stop - cols.start]
            product(m, i, cols, acc)
            copy(res[m][i][:, cols], acc)

        def rest(m, i, tag):
            acc = bank(tag)
            for cols in (middle, quarters[3]):
                product(m, i, cols, acc[:, cols])
            nc.scalar.copy(res[m][i][:, Q:S], acc[:, Q:S])

        early = [bank(0), bank(1)]
        firsts = ((0, G), (0, HN), (0, SH))
        for a, (m, i) in enumerate(firsts):
            product(m, i, quarters[0], early[a // 2][:, quarters[a % 2]])
        for a, (m, i) in enumerate(firsts):
            copy = nc.scalar.copy if a < 2 else nc.vector.tensor_copy
            copy(res[m][i][:, quarters[0]], early[a // 2][:, quarters[a % 2]])
        piece(0, G, middle, 2, nc.vector.tensor_copy)
        piece(0, G, quarters[3], 4, nc.scalar.copy)
        rest(0, HN, 5)

        gc = [keep.tile([P, V], F32, name="gc%d" % m) for m in range(2)]
        sc0 = keep.tile([P, V], F32, name="sc0", tag="sc")
        prod = [[keep.tile([P, V], F32, name="prod%d" % d) for d in range(2)]]
        left, right = halves = [slice(b * P, (b + 1) * P) for b in range(2)]

        def turn(acc, block, start, stop):
            nc.tensor.matmul(acc, block, ident[:], start=start, stop=stop, is_transpose=True)

        for blk in halves:
            nc.vector.tensor_copy(gc[0][:, blk], res[0][G][:].indirect(places(cen_t, blk.start, P)))
        nc.vector.tensor_tensor(prod[0][0][:, left], res[0][HN][:].indirect(places(pos_t[0], 0, P)), gc[0][:, left], MULT)
        nc.vector.tensor_tensor(prod[0][0][:, right], res[0][HN][:].indirect(places(pos_t[0], P, P)), gc[0][:, right], MULT)
        nc.vector.tensor_tensor(prod[0][1][:], res[0][HN][:].indirect(pos_t[1][:]), gc[0][:], MULT)
        rest(0, SH, 6)
        piece(1, G, slice(0, S), 7, nc.scalar.copy)
        nc.scalar.activation(sc0[:], res[0][SH][:].indirect(cen_t[:]), COPY)
        nc.scalar.activation(gc[1][:], res[1][G][:].indirect(cen_t[:]), COPY)
        piece(1, HN, slice(0, S), 5, nc.vector.tensor_copy)
        piece(1, SH, slice(0, H), 6, nc.vector.tensor_copy)
        piece(1, SH, slice(H, S), 4, nc.scalar.copy)

        act0 = keep.tile([P, 2, V], F32, name="act0")
        out0 = keep.tile([P, V], F32, name="out0", align_bytes=256)
        pre = [bank(b) for b in (2, 3)]
        for d in range(2):
            for b, blk in enumerate(halves):
                turn(pre[b][:, halves[d]], prod[0][d][:, blk], d == 0, False)
        for b, blk in enumerate(halves):
            for d in range(2):
                turn(pre[b][:, halves[d]], sc0[:, blk], False, d == 1)
        total = [bank(b) for b in (7, 0)]

        def finish(b):
            nc.scalar.activation(act0[:, b, :], pre[b][:, 0:V], SILU)
            for d in range(2):
                turn(total[b][:, 0:P], act0[:, b, halves[d]], d == 0, d == 1)

        finish(0)
        sc1 = keep.tile([P, V], F32, name="sc1", tag="sc")
        nc.scalar.activation(sc1[:], res[1][SH][:].indirect(cen_t[:]), COPY)
        finish(1)

        both = keep.tile([P, 2, V], F32, name="both")
        pre1 = keep.tile([P, 2, V], F32, name="pre1")
        act1 = keep.tile([P, 2, V], F32, name="act1")
        out1 = [keep.tile([P, P], F32, name="out1_%d" % b, align_bytes=256) for b in range(2)]
        for d in range(2):
            nc.vector.tensor_tensor(both[:, d, :], res[1][HN][:].indirect(pos_t[d][:]), gc[1][:], MULT)
        for d, blk in ((0, slice(0, V)), (1, left), (1, right)):
            nc.vector.tensor_tensor(pre1[:, d, blk], both[:, d, blk], sc1[:, blk], ADD)
            nc.scalar.activation(act1[:, d, blk], pre1[:, d, blk], SILU)
        for b, blk in enumerate(halves):
            nc.vector.tensor_copy(out0[:, blk], total[b][:, 0:P])
        nc.sync.dma_start(out[0:P, :], out0[:])
        for b, blk in enumerate(halves):
            nc.vector.tensor_tensor(out1[b][:], act1[:, 0, blk], act1[:, 1, blk], ADD)
            nc.sync.dma_start(out[P:2 * P, blk], out1[b][:])
